import numpy as np
import ml_dtypes


def mxq(x, axis, fmt="e4m3"):
    dtype, down = {"e4m3": (ml_dtypes.float8_e4m3fn, 7), "e5m2": (ml_dtypes.float8_e5m2, 14)}[fmt]
    v = np.moveaxis(np.asarray(x, np.float32).astype(ml_dtypes.bfloat16).astype(np.float64), axis, -1)
    blocks = v.reshape(v.shape[:-1] + (-1, 32))
    amax = np.abs(blocks).max(-1, keepdims=True)
    byte = np.maximum(np.where(amax > 0, np.frexp(amax)[1] - 1 + 127, 0) - down, 1)
    scale = np.exp2(byte - 127.0)
    codes = (blocks / scale).astype(np.float32).astype(dtype).astype(np.float64)
    return np.moveaxis((codes * scale).reshape(v.shape), -1, axis)


WIDE = False


def mx_kscale(k):
    if not WIDE:
        return np.ones(k)
    levels = np.array([10, -10, 5, -5, 0])
    if k % 512:
        return np.exp2(np.random.permutation(np.resize(levels, k // 32))).repeat(32)
    a = np.empty((k // 512, 16))
    for p in range(k // 512):
        a[p, :8] = np.random.permutation(np.resize(levels, 8))
        for g in range(8):
            far = levels[np.abs(levels - a[p, g]) >= 10]
            a[p, g + 8] = far[np.random.randint(len(far))]
    return np.exp2(a.ravel()).repeat(32)


def f64(x):
    return np.asarray(x).astype(np.float64)


def striped(idx):
    return np.tile(np.asarray(idx).reshape(-1, 16).T, (8, 1)).astype(np.uint16)


def unstriped(offs):
    return offs[:16].T.reshape(-1).astype(np.int64)


B, N, T, D, DV, NQ = 2, 512, 2048, 512, 256, 128
PAGE = 64


def setup_inputs():
    n = np.random.standard_normal
    pages = np.random.permutation(T // PAGE)[:B * N // PAGE]
    idx = (pages[:, None] * PAGE + np.arange(PAGE)[None, :]).reshape(-1)
    s = mx_kscale(D)[:, None]
    u = np.ones(T)
    u[idx] = mx_kscale(B * N)
    r = np.random.uniform(0.5, 2.0, T)
    k = n((D, T)) / s
    v = n((DV, T)) / (u * r)
    return {
        "qT": (n((B, D, NQ)) * s * (1.00 / np.sqrt(D))).astype(np.float32),
        "kT": k.astype(np.float32),
        "vT": v.astype(np.float32),
        "vs": np.tile(u * r, (128, 1)).astype(np.float32),
        "og": n((B, NQ, DV)).astype(np.float32),
        "offs": striped(idx),
    }


def reference(qT, kT, vT, vs, og, offs):
    idx = unstriped(offs)
    k = f64(kT)
    v = f64(vT)
    pick = lambda x: x[:, idx].reshape(x.shape[0], B, N).transpose(1, 0, 2)
    q = f64(qT)
    score = mxq(q, 1, "e4m3").transpose(0, 2, 1) @ mxq(pick(k), 1, "e4m3")
    p = 1.0 / (1.0 + np.exp(-score))
    w = p * pick(f64(vs))[:, :1, :]
    y = mxq(w, 2, "e4m3") @ mxq(pick(v).transpose(0, 2, 1), 1, "e4m3")
    y = y / 16.0
    y = y / (1.0 + np.exp(-f64(og)))
    return y

@@ -1,0 +1,210 @@
+from contextlib import ExitStack
+
+import concourse.mybir as mybir
+from concourse.masks import make_identity
+
+B, N, T, D, DV, NQ = 2, 512, 2048, 512, 256, 128
+P = 128
+PACK = 4
+
+F32 = mybir.dt.float32
+BF16 = mybir.dt.bfloat16
+U32 = mybir.dt.uint32
+U16 = mybir.dt.uint16
+U8 = mybir.dt.uint8
+FP8X4 = mybir.dt.float8_e4m3fn_x4
+SIGMOID = mybir.ActivationFunctionType.Sigmoid
+MULT = mybir.AluOpType.mult
+
+FLOPS = 2 * B * NQ * N * (D + DV)
+BYTES = 4 * (B * D * NQ + D * T + DV * T + T + 2 * B * NQ * DV) + 2 * P * (B * N // 16)
+
+
+def tile_attend_x_sigmoid_gate_kernel(tc, qT, kT, vT, vs, og, offs, out):
+    nc = tc.nc
+    cols = N // 16
+
+    with ExitStack() as ctx:
+        keep = ctx.enter_context(tc.tile_pool(name="keep", bufs=1))
+        psum = ctx.enter_context(tc.psum_pool(name="psum", bufs=1))
+
+        vs_win = keep.tile([P, T], F32, name="vs_win")
+        nc.vector.memset(vs_win[:], 0.0)
+        offsets = keep.tile([P, B * N // 16], U16, name="offsets")
+        nc.sync.dma_start(offsets[:], offs)
+
+        k_rows = kT.rearrange("(p j) t -> j p t", j=PACK)
+        k_win = []
+        for j in range(PACK):
+            w = keep.tile([P, T], F32, name=f"k_win{j}")
+            nc.sync.dma_start(w[:], k_rows[j])
+            k_win.append(w)
+            if j == 0:
+                nc.sync.dma_start(vs_win[0:1, :], vs[0:1, :])
+        q_raw = keep.tile([P, B, PACK * NQ], F32, name="q_raw")
+        nc.sync.dma_start(q_raw[:], qT.rearrange("b (p j) q -> p b (j q)", j=PACK))
+        v_win = []
+        for h in range(2):
+            w = keep.tile([P, T], F32, name=f"v_win{h}")
+            nc.sync.dma_start(w[:], vT[h * P : (h + 1) * P, :])
+            v_win.append(w)
+        og_sb = keep.tile([P, B, DV], F32, name="og_sb")
+        nc.sync.dma_start(og_sb[:], og.rearrange("b q e -> q b e"))
+
+        warm = keep.tile([P, 1], F32, name="warm")
+        nc.vector.memset(warm[:], 0.0)
+        nc.scalar.activation(warm[:], warm[:], SIGMOID)
+        ident_f = keep.tile([P, P], F32, name="ident_f")
+        make_identity(nc, ident_f[:])
+        ident_b = keep.tile([P, P], BF16, name="ident_b")
+        make_identity(nc, ident_b[:])
+
+        kg01 = keep.tile([P, 2, B * N], F32, name="kg01")
+        kg23 = keep.tile([P, 2, B * N], F32, name="kg23")
+        k_grouped = [keep.tile([P, PACK * N], BF16, name=f"k_grouped{b}", align_bytes=64) for b in range(B)]
+
+        def k_interleave(copy, src, b, j0):
+            dst = k_grouped[b][:].rearrange("p (t m j) -> p m t j", t=PACK, j=PACK)
+            copy(
+                out=dst[:, :, :, j0 : j0 + 2],
+                in_=src[:, :, b * N : (b + 1) * N].rearrange("p j (m t) -> p m t j", t=PACK),
+            )
+
+        nc.vector.tensor_copy(kg01[:, 0, :], k_win[0][:].indirect(offsets[:]))
+        nc.vector.tensor_copy(kg01[:, 1, :], k_win[1][:].indirect(offsets[:]))
+        vs_picked = keep.tile([P, B * N], F32, name="vs_picked")
+        nc.vector.tensor_copy(vs_picked[:], vs_win[:].indirect(offsets[:]))
+        for b in range(B):
+            k_interleave(nc.scalar.copy, kg01, b, 0)
+
+        vs_col = []
+        for b in range(B):
+            turned = psum.tile([P, PACK, P], F32, name="turned", tag="turned_vs", bufs=1)
+            picked = vs_picked[:, b * N : (b + 1) * N].rearrange("p (m t) -> p t m", t=PACK)
+            for t in range(PACK):
+                nc.tensor.transpose(turned[:, t, :], picked[:, t, :], ident_f[:])
+            c = keep.tile([P, 1, PACK], F32, name=f"vs_col{b}")
+            nc.vector.tensor_copy(out=c[:], in_=turned[:, :, 0:1].rearrange("p t o -> p o t"))
+            vs_col.append(c)
+
+        nc.vector.tensor_copy(kg23[:, 0, :], k_win[2][:].indirect(offsets[:]))
+
+        k_codes = [keep.tile([P, N], U32, name=f"k_codes{b}", align_bytes=64) for b in range(B)]
+        k_scales = [keep.tile([P, N], U8, name=f"k_scales{b}", align_bytes=64) for b in range(B)]
+        q_grouped = [keep.tile([P, NQ, PACK], BF16, name=f"q_grouped{b}", align_bytes=64) for b in range(B)]
+        q_codes = [keep.tile([P, NQ], U32, name=f"q_codes{b}", align_bytes=64) for b in range(B)]
+        q_scales = [keep.tile([P, NQ], U8, name=f"q_scales{b}", align_bytes=64) for b in range(B)]
+        p_sb = [keep.tile([P, NQ, PACK], F32, name=f"p_sb{b}") for b in range(B)]
+        w_grouped = [keep.tile([P, NQ, PACK], BF16, name=f"w_grouped{b}", align_bytes=64) for b in range(B)]
+        w_codes = [keep.tile([P, NQ], U32, name=f"w_codes{b}", align_bytes=64) for b in range(B)]
+        w_scales = [keep.tile([P, NQ], U8, name=f"w_scales{b}", align_bytes=64) for b in range(B)]
+        v_picked = [[keep.tile([P, N], BF16, name=f"v_picked{h}{b}") for b in range(B)] for h in range(2)]
+        v_grouped = [[keep.tile([P, P, PACK], BF16, name=f"v_grouped{h}{b}", align_bytes=64) for b in range(B)] for h in range(2)]
+        v_codes = [[keep.tile([P, P], U32, name=f"v_codes{h}{b}", align_bytes=64) for b in range(B)] for h in range(2)]
+        v_scales = [[keep.tile([P, P], U8, name=f"v_scales{h}{b}", align_bytes=64) for b in range(B)] for h in range(2)]
+
+        def quantize(codes, scales, grouped):
+            nc.vector.quantize_mx(out=codes[:].bitcast(FP8X4), scales=scales[:], in_=grouped)
+
+        def gather_k3(b):
+            nc.vector.tensor_copy(
+                kg23[:, 1, b * N : (b + 1) * N], k_win[3][:].indirect(offsets[:, b * cols : (b + 1) * cols])
+            )
+
+        def q_interleave(b):
+            nc.scalar.copy(out=q_grouped[b][:], in_=q_raw[:, b, :].rearrange("p (j q) -> p q j", j=PACK))
+
+        def q_quantize(b):
+            quantize(q_codes[b], q_scales[b], q_grouped[b][:].rearrange("p q j -> p (q j)"))
+
+        scores = [None, None]
+
+        def score(b):
+            bank = psum.tile([P, PACK, NQ], F32, name=f"score{b}")
+            for t in range(PACK):
+                c = slice(t * P, (t + 1) * P)
+                nc.tensor.matmul_mx(
+                    out=bank[:, t, :],
+                    lhsT=k_codes[b][:, c].bitcast(FP8X4),
+                    lhsT_scale=k_scales[b][:, c],
+                    rhs=q_codes[b][:].bitcast(FP8X4),
+                    rhs_scale=q_scales[b][:],
+                    start=True,
+                    stop=True,
+                )
+            nc.scalar.activation(p_sb[b][:], bank[:].rearrange("p t q -> p q t"), SIGMOID)
+
+        def weights(b):
+            nc.vector.tensor_tensor(
+                w_grouped[b][:], p_sb[b][:], vs_col[b][:].to_broadcast([P, NQ, PACK]), MULT
+            )
+
+        def w_quantize(b):
+            quantize(w_codes[b], w_scales[b], w_grouped[b][:].rearrange("p q j -> p (q j)"))
+
+        def gather_v(h, b):
+            nc.vector.tensor_copy(
+                v_picked[h][b][:].rearrange("p (t m) -> p m t", t=PACK),
+                v_win[h][:].indirect(offsets[:, b * cols : (b + 1) * cols]),
+            )
+
+        def turn_v(h, b):
+            bank = psum.tile([P, PACK, P], BF16, name="turned", tag="turned_v", bufs=3)
+            for t in range(PACK):
+                nc.tensor.transpose(bank[:, t, :], v_picked[h][b][:, t * P : (t + 1) * P], ident_b[:])
+            nc.scalar.copy(out=v_grouped[h][b][:], in_=bank[:].rearrange("p t e -> p e t"))
+
+        def v_quantize(h, b):
+            quantize(v_codes[h][b], v_scales[h][b], v_grouped[h][b][:].rearrange("p e t -> p (e t)"))
+
+        y_bank = [psum.tile([P, 2, P], F32, name=f"y_bank{b}") for b in range(B)]
+
+        def finish(h, b):
+            nc.tensor.matmul_mx(
+                out=y_bank[b][:, h, :],
+                lhsT=w_codes[b][:].bitcast(FP8X4),
+                lhsT_scale=w_scales[b][:],
+                rhs=v_codes[h][b][:].bitcast(FP8X4),
+                rhs_scale=v_scales[h][b][:],
+                start=True,
+                stop=True,
+            )
+            e = slice(h * P, (h + 1) * P)
+            o = keep.tile([P, P], F32, name=f"o{h}{b}")
+            nc.vector.scalar_tensor_tensor(o[:], y_bank[b][:, h, :], 1.0 / 16.0, gate[:, b, e], MULT, MULT)
+            nc.sync.dma_start(out[b, :, e], o[:])
+
+        gather_k3(0)
+        k_interleave(nc.vector.tensor_copy, kg23, 0, 2)
+        gather_k3(1)
+        k_interleave(nc.scalar.copy, kg23, 1, 2)
+        quantize(k_codes[0], k_scales[0], k_grouped[0][:])
+        for b in range(B):
+            q_interleave(b)
+        for b in range(B):
+            q_quantize(b)
+        score(0)
+        quantize(k_codes[1], k_scales[1], k_grouped[1][:])
+        score(1)
+        gather_v(0, 0)
+        turn_v(0, 0)
+        gather_v(0, 1)
+        turn_v(0, 1)
+        weights(0)
+        w_quantize(0)
+        weights(1)
+        w_quantize(1)
+        v_quantize(0, 0)
+        v_quantize(0, 1)
+        gate = keep.tile([P, B, DV], F32, name="gate")
+        gather_v(1, 0)
+        turn_v(1, 0)
+        nc.scalar.activation(gate[:], og_sb[:], SIGMOID)
+        finish(0, 0)
+        finish(0, 1)
+        gather_v(1, 1)
+        turn_v(1, 1)
+        v_quantize(1, 0)
+        finish(1, 0)
+        v_quantize(1, 1)
+        finish(1, 1)

@@ -23,103 +23,90 @@ BYTES = 4 * (B * D * NQ + D * T + DV * T + T + 2 * B * NQ * DV) + 2 * P * (B * N
 def tile_attend_x_sigmoid_gate_kernel(tc, qT, kT, vT, vs, og, offs, out):
     nc = tc.nc
     cols = N // 16
+    last = P - 1
 
     with ExitStack() as ctx:
         keep = ctx.enter_context(tc.tile_pool(name="keep", bufs=1))
         psum = ctx.enter_context(tc.psum_pool(name="psum", bufs=1))
 
-        vs_win = keep.tile([P, T], F32, name="vs_win")
-        nc.vector.memset(vs_win[:], 0.0)
         offsets = keep.tile([P, B * N // 16], U16, name="offsets")
         nc.sync.dma_start(offsets[:], offs)
+        vs_win = keep.tile([P, T], F32, name="vs_win")
+        nc.sync.dma_start(vs_win[last:P, :], vs[0:1, :])
+        nc.gpsimd.memset(vs_win[0:last, T // 2 : T], 0.0)
+        nc.vector.memset(vs_win[0:last, 0 : T // 2], 0.0)
 
         k_rows = kT.rearrange("(p j) t -> j p t", j=PACK)
-        k_win = []
-        for j in range(PACK):
-            w = keep.tile([P, T], F32, name=f"k_win{j}")
-            nc.sync.dma_start(w[:], k_rows[j])
-            k_win.append(w)
-            if j == 0:
-                nc.sync.dma_start(vs_win[0:1, :], vs[0:1, :])
+        k_win = [keep.tile([P, T], F32, name=f"k_win{j}") for j in range(PACK)]
         q_raw = keep.tile([P, B, PACK * NQ], F32, name="q_raw")
+        for j in range(PACK - 1):
+            nc.sync.dma_start(k_win[j][:], k_rows[j])
         nc.sync.dma_start(q_raw[:], qT.rearrange("b (p j) q -> p b (j q)", j=PACK))
-        v_win = []
-        for h in range(2):
-            w = keep.tile([P, T], F32, name=f"v_win{h}")
-            nc.sync.dma_start(w[:], vT[h * P : (h + 1) * P, :])
-            v_win.append(w)
+        nc.sync.dma_start(k_win[PACK - 1][:], k_rows[PACK - 1])
+        v_win = [keep.tile([P, T], F32, name=f"v_win{h}") for h in range(2)]
+        nc.sync.dma_start(v_win[0][:], vT[0:P, :])
+        nc.sync.dma_start(v_win[1][:], vT[P:DV, :])
         og_sb = keep.tile([P, B, DV], F32, name="og_sb")
         nc.sync.dma_start(og_sb[:], og.rearrange("b q e -> q b e"))
 
         warm = keep.tile([P, 1], F32, name="warm")
         nc.vector.memset(warm[:], 0.0)
         nc.scalar.activation(warm[:], warm[:], SIGMOID)
-        ident_f = keep.tile([P, P], F32, name="ident_f")
-        make_identity(nc, ident_f[:])
-        ident_b = keep.tile([P, P], BF16, name="ident_b")
-        make_identity(nc, ident_b[:])
+        ident = keep.tile([P, P], F32, name="ident")
+        make_identity(nc, ident[:])
 
-        kg01 = keep.tile([P, 2, B * N], F32, name="kg01")
-        kg23 = keep.tile([P, 2, B * N], F32, name="kg23")
-        k_grouped = [keep.tile([P, PACK * N], BF16, name=f"k_grouped{b}", align_bytes=64) for b in range(B)]
+        def listed(window, b):
+            return window[:].indirect(offsets[:, b * cols : (b + 1) * cols])
 
-        def k_interleave(copy, src, b, j0):
-            dst = k_grouped[b][:].rearrange("p (t m j) -> p m t j", t=PACK, j=PACK)
-            copy(
-                out=dst[:, :, :, j0 : j0 + 2],
-                in_=src[:, :, b * N : (b + 1) * N].rearrange("p j (m t) -> p m t j", t=PACK),
-            )
+        def quantize(codes, scales, grouped):
+            nc.vector.quantize_mx(out=codes.bitcast(FP8X4), scales=scales, in_=grouped)
 
-        nc.vector.tensor_copy(kg01[:, 0, :], k_win[0][:].indirect(offsets[:]))
-        nc.vector.tensor_copy(kg01[:, 1, :], k_win[1][:].indirect(offsets[:]))
+        def turn_bank():
+            return psum.tile([P, PACK, P], F32, name="turned", tag="turned", bufs=3)
+
         vs_picked = keep.tile([P, B * N], F32, name="vs_picked")
         nc.vector.tensor_copy(vs_picked[:], vs_win[:].indirect(offsets[:]))
-        for b in range(B):
-            k_interleave(nc.scalar.copy, kg01, b, 0)
-
         vs_col = []
         for b in range(B):
-            turned = psum.tile([P, PACK, P], F32, name="turned", tag="turned_vs", bufs=1)
+            turned = turn_bank()
             picked = vs_picked[:, b * N : (b + 1) * N].rearrange("p (m t) -> p t m", t=PACK)
             for t in range(PACK):
-                nc.tensor.transpose(turned[:, t, :], picked[:, t, :], ident_f[:])
+                nc.tensor.transpose(turned[:, t, :], picked[:, t, :], ident[:])
             c = keep.tile([P, 1, PACK], F32, name=f"vs_col{b}")
-            nc.vector.tensor_copy(out=c[:], in_=turned[:, :, 0:1].rearrange("p t o -> p o t"))
+            nc.scalar.copy(out=c[:], in_=turned[:, :, last:P].rearrange("p t o -> p o t"))
             vs_col.append(c)
 
-        nc.vector.tensor_copy(kg23[:, 0, :], k_win[2][:].indirect(offsets[:]))
+        k_picked = keep.tile([P, PACK, B, N], BF16, name="k_picked")
+        k_grouped = [
+            keep.tile([P, PACK * N], BF16, name=f"k_grouped{b}", tag=f"k_grouped{b}", align_bytes=64) for b in range(B)
+        ]
+        for j in range(PACK - 1):
+            nc.vector.tensor_copy(
+                k_picked[:, j, :, :].rearrange("p b (t m) -> p b m t", t=PACK), k_win[j][:].indirect(offsets[:])
+            )
+        for b in range(B):
+            nc.vector.tensor_copy(
+                k_picked[:, PACK - 1, b, :].rearrange("p (t m) -> p m t", t=PACK), listed(k_win[PACK - 1], b)
+            )
+        for b in range(B):
+            nc.scalar.copy(
+                out=k_grouped[b][:].rearrange("p (c i j) -> p c j i", i=4, j=PACK),
+                in_=k_picked[:, :, b, :].rearrange("p j (c i) -> p c j i", i=4),
+            )
+
+        q_grouped = keep.tile([P, B, NQ, PACK], BF16, name="q_grouped", align_bytes=64)
+        q_codes = keep.tile([P, B * NQ], U32, name="q_codes", align_bytes=64)
+        q_scales = keep.tile([P, B * NQ], U8, name="q_scales", align_bytes=64)
+        nc.scalar.copy(out=q_grouped[:], in_=q_raw[:].rearrange("p b (j q) -> p b q j", j=PACK))
 
         k_codes = [keep.tile([P, N], U32, name=f"k_codes{b}", align_bytes=64) for b in range(B)]
         k_scales = [keep.tile([P, N], U8, name=f"k_scales{b}", align_bytes=64) for b in range(B)]
-        q_grouped = [keep.tile([P, NQ, PACK], BF16, name=f"q_grouped{b}", align_bytes=64) for b in range(B)]
-        q_codes = [keep.tile([P, NQ], U32, name=f"q_codes{b}", align_bytes=64) for b in range(B)]
-        q_scales = [keep.tile([P, NQ], U8, name=f"q_scales{b}", align_bytes=64) for b in range(B)]
+        for b in range(B):
+            quantize(k_codes[b][:], k_scales[b][:], k_grouped[b][:])
+        quantize(q_codes[:], q_scales[:], q_grouped[:].rearrange("p b q j -> p (b q j)"))
+
         p_sb = [keep.tile([P, NQ, PACK], F32, name=f"p_sb{b}") for b in range(B)]
-        w_grouped = [keep.tile([P, NQ, PACK], BF16, name=f"w_grouped{b}", align_bytes=64) for b in range(B)]
-        w_codes = [keep.tile([P, NQ], U32, name=f"w_codes{b}", align_bytes=64) for b in range(B)]
-        w_scales = [keep.tile([P, NQ], U8, name=f"w_scales{b}", align_bytes=64) for b in range(B)]
-        v_picked = [[keep.tile([P, N], BF16, name=f"v_picked{h}{b}") for b in range(B)] for h in range(2)]
-        v_grouped = [[keep.tile([P, P, PACK], BF16, name=f"v_grouped{h}{b}", align_bytes=64) for b in range(B)] for h in range(2)]
-        v_codes = [[keep.tile([P, P], U32, name=f"v_codes{h}{b}", align_bytes=64) for b in range(B)] for h in range(2)]
-        v_scales = [[keep.tile([P, P], U8, name=f"v_scales{h}{b}", align_bytes=64) for b in range(B)] for h in range(2)]
-
-        def quantize(codes, scales, grouped):
-            nc.vector.quantize_mx(out=codes[:].bitcast(FP8X4), scales=scales[:], in_=grouped)
-
-        def gather_k3(b):
-            nc.vector.tensor_copy(
-                kg23[:, 1, b * N : (b + 1) * N], k_win[3][:].indirect(offsets[:, b * cols : (b + 1) * cols])
-            )
-
-        def q_interleave(b):
-            nc.scalar.copy(out=q_grouped[b][:], in_=q_raw[:, b, :].rearrange("p (j q) -> p q j", j=PACK))
-
-        def q_quantize(b):
-            quantize(q_codes[b], q_scales[b], q_grouped[b][:].rearrange("p q j -> p (q j)"))
-
-        scores = [None, None]
-
-        def score(b):
+        for b in range(B):
             bank = psum.tile([P, PACK, NQ], F32, name=f"score{b}")
             for t in range(PACK):
                 c = slice(t * P, (t + 1) * P)
@@ -127,84 +114,82 @@ def tile_attend_x_sigmoid_gate_kernel(tc, qT, kT, vT, vs, og, offs, out):
                     out=bank[:, t, :],
                     lhsT=k_codes[b][:, c].bitcast(FP8X4),
                     lhsT_scale=k_scales[b][:, c],
-                    rhs=q_codes[b][:].bitcast(FP8X4),
-                    rhs_scale=q_scales[b][:],
+                    rhs=q_codes[:, b * NQ : (b + 1) * NQ].bitcast(FP8X4),
+                    rhs_scale=q_scales[:, b * NQ : (b + 1) * NQ],
                     start=True,
                     stop=True,
                 )
             nc.scalar.activation(p_sb[b][:], bank[:].rearrange("p t q -> p q t"), SIGMOID)
 
-        def weights(b):
-            nc.vector.tensor_tensor(
-                w_grouped[b][:], p_sb[b][:], vs_col[b][:].to_broadcast([P, NQ, PACK]), MULT
-            )
-
-        def w_quantize(b):
-            quantize(w_codes[b], w_scales[b], w_grouped[b][:].rearrange("p q j -> p (q j)"))
-
         def gather_v(h, b):
-            nc.vector.tensor_copy(
-                v_picked[h][b][:].rearrange("p (t m) -> p m t", t=PACK),
-                v_win[h][:].indirect(offsets[:, b * cols : (b + 1) * cols]),
+            tag = "k_grouped1" if (h, b) == (1, 1) else f"v_picked{h}{b}"
+            picked = keep.tile([P, N], BF16, name=f"v_picked{h}{b}", tag=tag, align_bytes=64)
+            nc.vector.tensor_copy(picked[:].rearrange("p (u m r) -> p m u r", u=2, r=2), listed(v_win[h], b))
+            return picked[:].bitcast(F32)
+
+        def turn_v(words, bank):
+            for u in range(2):
+                nc.tensor.transpose(bank[:, u, :], words[:, u * P : (u + 1) * P], ident[:])
+
+        bank0 = turn_bank()
+        for b in range(B):
+            turn_v(gather_v(0, b), bank0[:, 2 * b : 2 * b + 2, :])
+        v0_grouped = keep.tile([P, B * P * PACK], BF16, name="v0_grouped", align_bytes=64)
+        nc.scalar.copy(
+            out=v0_grouped[:].bitcast(F32).rearrange("p (b e u) -> p b e u", b=B, u=2),
+            in_=bank0[:].rearrange("p (b u) e -> p b e u", u=2),
+        )
+
+        v1_grouped = []
+        for b in range(B):
+            bank = turn_bank()
+            turn_v(gather_v(1, b), bank[:, 0:2, :])
+            g = keep.tile([P, P * PACK], BF16, name=f"v1_grouped{b}", align_bytes=64)
+            nc.scalar.copy(
+                out=g[:].bitcast(F32).rearrange("p (e u) -> p e u", u=2),
+                in_=bank[:, 0:2, :].rearrange("p u e -> p e u"),
             )
+            v1_grouped.append(g)
 
-        def turn_v(h, b):
-            bank = psum.tile([P, PACK, P], BF16, name="turned", tag="turned_v", bufs=3)
-            for t in range(PACK):
-                nc.tensor.transpose(bank[:, t, :], v_picked[h][b][:, t * P : (t + 1) * P], ident_b[:])
-            nc.scalar.copy(out=v_grouped[h][b][:], in_=bank[:].rearrange("p t e -> p e t"))
+        w_codes = [keep.tile([P, NQ], U32, name=f"w_codes{b}", align_bytes=64) for b in range(B)]
+        w_scales = [keep.tile([P, NQ], U8, name=f"w_scales{b}", align_bytes=64) for b in range(B)]
+        w_grouped = [keep.tile([P, NQ, PACK], BF16, name=f"w_grouped{b}", align_bytes=64) for b in range(B)]
+        for b in range(B):
+            nc.vector.tensor_tensor(w_grouped[b][:], p_sb[b][:], vs_col[b][:].to_broadcast([P, NQ, PACK]), MULT)
+        for b in range(B):
+            quantize(w_codes[b][:], w_scales[b][:], w_grouped[b][:].rearrange("p q j -> p (q j)"))
 
-        def v_quantize(h, b):
-            quantize(v_codes[h][b], v_scales[h][b], v_grouped[h][b][:].rearrange("p e t -> p (e t)"))
+        gate = keep.tile([P, B, DV], F32, name="gate")
+        nc.scalar.activation(gate[:], og_sb[:], SIGMOID)
 
-        y_bank = [psum.tile([P, 2, P], F32, name=f"y_bank{b}") for b in range(B)]
-
-        def finish(h, b):
+        def weigh(y, b, codes, scales):
             nc.tensor.matmul_mx(
-                out=y_bank[b][:, h, :],
+                out=y,
                 lhsT=w_codes[b][:].bitcast(FP8X4),
                 lhsT_scale=w_scales[b][:],
-                rhs=v_codes[h][b][:].bitcast(FP8X4),
-                rhs_scale=v_scales[h][b][:],
+                rhs=codes.bitcast(FP8X4),
+                rhs_scale=scales,
                 start=True,
                 stop=True,
             )
-            e = slice(h * P, (h + 1) * P)
-            o = keep.tile([P, P], F32, name=f"o{h}{b}")
-            nc.vector.scalar_tensor_tensor(o[:], y_bank[b][:, h, :], 1.0 / 16.0, gate[:, b, e], MULT, MULT)
-            nc.sync.dma_start(out[b, :, e], o[:])
 
-        gather_k3(0)
-        k_interleave(nc.vector.tensor_copy, kg23, 0, 2)
-        gather_k3(1)
-        k_interleave(nc.scalar.copy, kg23, 1, 2)
-        quantize(k_codes[0], k_scales[0], k_grouped[0][:])
+        out_q = out.rearrange("b q e -> q b e")
+        v0_codes = keep.tile([P, B * P], U32, name="v0_codes", align_bytes=64)
+        v0_scales = keep.tile([P, B * P], U8, name="v0_scales", align_bytes=64)
+        quantize(v0_codes[:], v0_scales[:], v0_grouped[:])
+        y0 = psum.tile([P, B, P], F32, name="y0")
         for b in range(B):
-            q_interleave(b)
+            weigh(y0[:, b, :], b, v0_codes[:, b * P : (b + 1) * P], v0_scales[:, b * P : (b + 1) * P])
+        o0 = keep.tile([P, B, P], F32, name="o0")
+        nc.vector.scalar_tensor_tensor(o0[:], y0[:], 1.0 / 16.0, gate[:, :, 0:P], MULT, MULT)
+        nc.sync.dma_start(out_q[:, :, 0:P], o0[:])
+
         for b in range(B):
-            q_quantize(b)
-        score(0)
-        quantize(k_codes[1], k_scales[1], k_grouped[1][:])
-        score(1)
-        gather_v(0, 0)
-        turn_v(0, 0)
-        gather_v(0, 1)
-        turn_v(0, 1)
-        weights(0)
-        w_quantize(0)
-        weights(1)
-        w_quantize(1)
-        v_quantize(0, 0)
-        v_quantize(0, 1)
-        gate = keep.tile([P, B, DV], F32, name="gate")
-        gather_v(1, 0)
-        turn_v(1, 0)
-        nc.scalar.activation(gate[:], og_sb[:], SIGMOID)
-        finish(0, 0)
-        finish(0, 1)
-        gather_v(1, 1)
-        turn_v(1, 1)
-        v_quantize(1, 0)
-        finish(1, 0)
-        v_quantize(1, 1)
-        finish(1, 1)
+            codes = keep.tile([P, P], U32, name=f"v1_codes{b}", align_bytes=64)
+            scales = keep.tile([P, P], U8, name=f"v1_scales{b}", align_bytes=64)
+            quantize(codes[:], scales[:], v1_grouped[b][:])
+            y1 = psum.tile([P, P], F32, name=f"y1{b}")
+            weigh(y1[:], b, codes[:], scales[:])
+            o1 = keep.tile([P, P], F32, name=f"o1{b}")
+            nc.vector.scalar_tensor_tensor(o1[:], y1[:], 1.0 / 16.0, gate[:, b, P:DV], MULT, MULT)
+            nc.sync.dma_start(out[b, :, P:DV], o1[:])

@@ -10,10 +10,12 @@ PACK = 4
 F32 = mybir.dt.float32
 BF16 = mybir.dt.bfloat16
 U32 = mybir.dt.uint32
+I32 = mybir.dt.int32
 U16 = mybir.dt.uint16
 U8 = mybir.dt.uint8
 FP8X4 = mybir.dt.float8_e4m3fn_x4
 SIGMOID = mybir.ActivationFunctionType.Sigmoid
+COPY = mybir.ActivationFunctionType.Copy
 MULT = mybir.AluOpType.mult
 
 FLOPS = 2 * B * NQ * N * (D + DV)
@@ -36,16 +38,20 @@ def tile_attend_x_sigmoid_gate_kernel(tc, qT, kT, vT, vs, og, offs, out):
         nc.gpsimd.memset(vs_win[0:last, T // 2 : T], 0.0)
         nc.vector.memset(vs_win[0:last, 0 : T // 2], 0.0)
 
-        k_rows = kT.rearrange("(p j) t -> j p t", j=PACK)
-        k_win = [keep.tile([P, T], F32, name=f"k_win{j}") for j in range(PACK)]
+        k_rows = kT.rearrange("(p j) t -> p j t", j=PACK)
+        key_chunks = [[(0, 1024), (1024, T)], [(0, 1024), (1024, 1536), (1536, T)]]
+        k_raw = {}
+        for u in range(2):
+            for lo, hi in key_chunks[u]:
+                k_raw[u, lo] = keep.tile([P, 2, hi - lo], F32, name=f"k_raw{u}_{lo}")
+                nc.sync.dma_start(k_raw[u, lo][:], k_rows[:, 2 * u : 2 * u + 2, lo:hi])
         q_raw = keep.tile([P, B, PACK * NQ], F32, name="q_raw")
-        for j in range(PACK - 1):
-            nc.sync.dma_start(k_win[j][:], k_rows[j])
         nc.sync.dma_start(q_raw[:], qT.rearrange("b (p j) q -> p b (j q)", j=PACK))
-        nc.sync.dma_start(k_win[PACK - 1][:], k_rows[PACK - 1])
-        v_win = [keep.tile([P, T], F32, name=f"v_win{h}") for h in range(2)]
-        nc.sync.dma_start(v_win[0][:], vT[0:P, :])
-        nc.sync.dma_start(v_win[1][:], vT[P:DV, :])
+        v0_raw = [keep.tile([P, T // 2], F32, name=f"v0_raw{c}", tag=f"v0_raw{c}") for c in range(2)]
+        for c in range(2):
+            nc.sync.dma_start(v0_raw[c][:], vT[0:P, c * T // 2 : (c + 1) * T // 2])
+        v1_win = keep.tile([P, T], F32, name="v1_win")
+        nc.sync.dma_start(v1_win[:], vT[P:DV, :])
         og_sb = keep.tile([P, B, DV], F32, name="og_sb")
         nc.sync.dma_start(og_sb[:], og.rearrange("b q e -> q b e"))
 
@@ -76,22 +82,33 @@ def tile_attend_x_sigmoid_gate_kernel(tc, qT, kT, vT, vs, og, offs, out):
             nc.scalar.copy(out=c[:], in_=turned[:, :, last:P].rearrange("p t o -> p o t"))
             vs_col.append(c)
 
-        k_picked = keep.tile([P, PACK, B, N], BF16, name="k_picked")
+        k_win = [keep.tile([P, T], U32, name=f"k_win{u}") for u in range(2)]
+
+        def cast_pairs(u, lo, hi, share):
+            pairs = k_win[u][:, lo:hi].bitcast(BF16).rearrange("p (t r) -> p t r", r=2)
+            rows = k_raw[u, lo][:].rearrange("p r t -> p t r")
+            nc.scalar.activation(pairs[:, 0:share, :], rows[:, 0:share, :], COPY)
+            nc.vector.tensor_copy(pairs[:, share:, :], rows[:, share:, :])
+
+        k_both = [keep.tile([P, 2, N], U32, name=f"k_both{b}") for b in range(B)]
+
+        def gather_k(u):
+            for b in range(B):
+                nc.vector.tensor_copy(k_both[b][:, u, :].rearrange("p (t m) -> p m t", t=PACK), listed(k_win[u], b))
+
+        cast_pairs(0, 0, 1024, 768)
+        cast_pairs(0, 1024, T, 352)
+        gather_k(0)
+        for lo, hi in key_chunks[1]:
+            cast_pairs(1, lo, hi, (hi - lo) * 11 // 32)
+        gather_k(1)
         k_grouped = [
             keep.tile([P, PACK * N], BF16, name=f"k_grouped{b}", tag=f"k_grouped{b}", align_bytes=64) for b in range(B)
         ]
-        for j in range(PACK - 1):
-            nc.vector.tensor_copy(
-                k_picked[:, j, :, :].rearrange("p b (t m) -> p b m t", t=PACK), k_win[j][:].indirect(offsets[:])
-            )
         for b in range(B):
             nc.vector.tensor_copy(
-                k_picked[:, PACK - 1, b, :].rearrange("p (t m) -> p m t", t=PACK), listed(k_win[PACK - 1], b)
-            )
-        for b in range(B):
-            nc.scalar.copy(
-                out=k_grouped[b][:].rearrange("p (c i j) -> p c j i", i=4, j=PACK),
-                in_=k_picked[:, :, b, :].rearrange("p j (c i) -> p c j i", i=4),
+                k_grouped[b][:].bitcast(I32).rearrange("p (c u) -> p c u", u=2),
+                k_both[b][:].bitcast(I32).rearrange("p u c -> p c u"),
             )
 
         q_grouped = keep.tile([P, B, NQ, PACK], BF16, name="q_grouped", align_bytes=64)
@@ -105,7 +122,17 @@ def tile_attend_x_sigmoid_gate_kernel(tc, qT, kT, vT, vs, og, offs, out):
             quantize(k_codes[b][:], k_scales[b][:], k_grouped[b][:])
         quantize(q_codes[:], q_scales[:], q_grouped[:].rearrange("p b q j -> p (b q j)"))
 
-        p_sb = [keep.tile([P, NQ, PACK], F32, name=f"p_sb{b}") for b in range(B)]
+        v0_win = keep.tile([P, T], BF16, name="v0_win")
+        for c in range(2):
+            nc.scalar.activation(v0_win[:, c * T // 2 : (c + 1) * T // 2], v0_raw[c][:], COPY)
+
+        def paired(picked):
+            return picked[:].rearrange("p (u m r) -> p m u r", u=2, r=2)
+
+        v0_picked = [keep.tile([P, N], BF16, name=f"v0_picked{b}", tag=f"v0_picked{b}") for b in range(B)]
+        nc.scalar.activation(paired(v0_picked[0]), listed(v0_win, 0), COPY)
+
+        p_sb = keep.tile([P, B, NQ, PACK], F32, name="p_sb", tag="v0_raw1")
         for b in range(B):
             bank = psum.tile([P, PACK, NQ], F32, name=f"score{b}")
             for t in range(PACK):
@@ -119,31 +146,20 @@ def tile_attend_x_sigmoid_gate_kernel(tc, qT, kT, vT, vs, og, offs, out):
                     start=True,
                     stop=True,
                 )
-            nc.scalar.activation(p_sb[b][:], bank[:].rearrange("p t q -> p q t"), SIGMOID)
+            nc.scalar.activation(p_sb[:, b, :, :], bank[:].rearrange("p t q -> p q t"), SIGMOID)
 
-        def gather_v(h, b):
-            tag = "k_grouped1" if (h, b) == (1, 1) else f"v_picked{h}{b}"
-            picked = keep.tile([P, N], BF16, name=f"v_picked{h}{b}", tag=tag, align_bytes=64)
-            nc.vector.tensor_copy(picked[:].rearrange("p (u m r) -> p m u r", u=2, r=2), listed(v_win[h], b))
-            return picked[:].bitcast(F32)
+        nc.scalar.activation(paired(v0_picked[1]), listed(v0_win, 1), COPY)
 
         def turn_v(words, bank):
             for u in range(2):
                 nc.tensor.transpose(bank[:, u, :], words[:, u * P : (u + 1) * P], ident[:])
 
-        bank0 = turn_bank()
-        for b in range(B):
-            turn_v(gather_v(0, b), bank0[:, 2 * b : 2 * b + 2, :])
-        v0_grouped = keep.tile([P, B * P * PACK], BF16, name="v0_grouped", align_bytes=64)
-        nc.scalar.copy(
-            out=v0_grouped[:].bitcast(F32).rearrange("p (b e u) -> p b e u", b=B, u=2),
-            in_=bank0[:].rearrange("p (b u) e -> p b e u", u=2),
-        )
-
+        v1_picked = [keep.tile([P, N], BF16, name=f"v1_picked{b}", tag=f"v1_picked{b}", align_bytes=64) for b in range(B)]
         v1_grouped = []
         for b in range(B):
+            nc.vector.tensor_copy(paired(v1_picked[b]), listed(v1_win, b))
             bank = turn_bank()
-            turn_v(gather_v(1, b), bank[:, 0:2, :])
+            turn_v(v1_picked[b][:].bitcast(F32), bank[:, 0:2, :])
             g = keep.tile([P, P * PACK], BF16, name=f"v1_grouped{b}", align_bytes=64)
             nc.scalar.copy(
                 out=g[:].bitcast(F32).rearrange("p (e u) -> p e u", u=2),
@@ -151,15 +167,26 @@ def tile_attend_x_sigmoid_gate_kernel(tc, qT, kT, vT, vs, og, offs, out):
             )
             v1_grouped.append(g)
 
+        bank0 = turn_bank()
+        for b in range(B):
+            turn_v(v0_picked[b][:].bitcast(F32), bank0[:, 2 * b : 2 * b + 2, :])
+        v0_grouped = keep.tile([P, B * P * PACK], BF16, name="v0_grouped", align_bytes=64)
+        nc.scalar.copy(
+            out=v0_grouped[:].bitcast(F32).rearrange("p (b e u) -> p b e u", b=B, u=2),
+            in_=bank0[:].rearrange("p (b u) e -> p b e u", u=2),
+        )
+
         w_codes = [keep.tile([P, NQ], U32, name=f"w_codes{b}", align_bytes=64) for b in range(B)]
         w_scales = [keep.tile([P, NQ], U8, name=f"w_scales{b}", align_bytes=64) for b in range(B)]
-        w_grouped = [keep.tile([P, NQ, PACK], BF16, name=f"w_grouped{b}", align_bytes=64) for b in range(B)]
+        w_grouped = [
+            keep.tile([P, NQ, PACK], BF16, name=f"w_grouped{b}", tag=f"v1_picked{b}", align_bytes=64) for b in range(B)
+        ]
         for b in range(B):
-            nc.vector.tensor_tensor(w_grouped[b][:], p_sb[b][:], vs_col[b][:].to_broadcast([P, NQ, PACK]), MULT)
+            nc.vector.tensor_tensor(w_grouped[b][:], p_sb[:, b, :, :], vs_col[b][:].to_broadcast([P, NQ, PACK]), MULT)
         for b in range(B):
             quantize(w_codes[b][:], w_scales[b][:], w_grouped[b][:].rearrange("p q j -> p (q j)"))
 
-        gate = keep.tile([P, B, DV], F32, name="gate")
+        gate = keep.tile([P, B, DV], F32, name="gate", tag="v0_picked1")
         nc.scalar.activation(gate[:], og_sb[:], SIGMOID)
 
         def weigh(y, b, codes, scales):
@@ -174,16 +201,6 @@ def tile_attend_x_sigmoid_gate_kernel(tc, qT, kT, vT, vs, og, offs, out):
             )
 
         out_q = out.rearrange("b q e -> q b e")
-        v0_codes = keep.tile([P, B * P], U32, name="v0_codes", align_bytes=64)
-        v0_scales = keep.tile([P, B * P], U8, name="v0_scales", align_bytes=64)
-        quantize(v0_codes[:], v0_scales[:], v0_grouped[:])
-        y0 = psum.tile([P, B, P], F32, name="y0")
-        for b in range(B):
-            weigh(y0[:, b, :], b, v0_codes[:, b * P : (b + 1) * P], v0_scales[:, b * P : (b + 1) * P])
-        o0 = keep.tile([P, B, P], F32, name="o0")
-        nc.vector.scalar_tensor_tensor(o0[:], y0[:], 1.0 / 16.0, gate[:, :, 0:P], MULT, MULT)
-        nc.sync.dma_start(out_q[:, :, 0:P], o0[:])
-
         for b in range(B):
             codes = keep.tile([P, P], U32, name=f"v1_codes{b}", align_bytes=64)
             scales = keep.tile([P, P], U8, name=f"v1_scales{b}", align_bytes=64)
@@ -193,3 +210,13 @@ def tile_attend_x_sigmoid_gate_kernel(tc, qT, kT, vT, vs, og, offs, out):
             o1 = keep.tile([P, P], F32, name=f"o1{b}")
             nc.vector.scalar_tensor_tensor(o1[:], y1[:], 1.0 / 16.0, gate[:, b, P:DV], MULT, MULT)
             nc.sync.dma_start(out[b, :, P:DV], o1[:])
+
+        v0_codes = keep.tile([P, B * P], U32, name="v0_codes", align_bytes=64)
+        v0_scales = keep.tile([P, B * P], U8, name="v0_scales", align_bytes=64)
+        quantize(v0_codes[:], v0_scales[:], v0_grouped[:])
+        y0 = psum.tile([P, B, P], F32, name="y0")
+        for b in range(B):
+            weigh(y0[:, b, :], b, v0_codes[:, b * P : (b + 1) * P], v0_scales[:, b * P : (b + 1) * P])
+        o0 = keep.tile([P, B, P], F32, name="o0")
+        nc.vector.scalar_tensor_tensor(o0[:], y0[:], 1.0 / 16.0, gate[:, :, 0:P], MULT, MULT)
+        nc.sync.dma_start(out_q[:, :, 0:P], o0[:])

@@ -40,17 +40,17 @@ def tile_attend_x_sigmoid_gate_kernel(tc, qT, kT, vT, vs, og, offs, out):
 
         k_rows = kT.rearrange("(p j) t -> p j t", j=PACK)
         key_chunks = [[(0, 1024), (1024, T)], [(0, 1024), (1024, 1536), (1536, T)]]
-        k_raw = {}
+        k_raw = [keep.tile([P, 2, T], F32, name=f"k_raw{u}") for u in range(2)]
         for u in range(2):
+            nc.sync.dma_start(k_raw[u][:, 0, :], k_rows[:, 2 * u, :])
             for lo, hi in key_chunks[u]:
-                k_raw[u, lo] = keep.tile([P, 2, hi - lo], F32, name=f"k_raw{u}_{lo}")
-                nc.sync.dma_start(k_raw[u, lo][:], k_rows[:, 2 * u : 2 * u + 2, lo:hi])
+                nc.sync.dma_start(k_raw[u][:, 1, lo:hi], k_rows[:, 2 * u + 1, lo:hi])
         q_raw = keep.tile([P, B, PACK * NQ], F32, name="q_raw")
         nc.sync.dma_start(q_raw[:], qT.rearrange("b (p j) q -> p b (j q)", j=PACK))
         v0_raw = [keep.tile([P, T // 2], F32, name=f"v0_raw{c}", tag=f"v0_raw{c}") for c in range(2)]
         for c in range(2):
             nc.sync.dma_start(v0_raw[c][:], vT[0:P, c * T // 2 : (c + 1) * T // 2])
-        v1_win = keep.tile([P, T], F32, name="v1_win")
+        v1_win = keep.tile([P, T], F32, name="v1_win", tag="v1_win", align_bytes=64)
         nc.sync.dma_start(v1_win[:], vT[P:DV, :])
         og_sb = keep.tile([P, B, DV], F32, name="og_sb")
         nc.sync.dma_start(og_sb[:], og.rearrange("b q e -> q b e"))
@@ -72,21 +72,19 @@ def tile_attend_x_sigmoid_gate_kernel(tc, qT, kT, vT, vs, og, offs, out):
 
         vs_picked = keep.tile([P, B * N], F32, name="vs_picked")
         nc.vector.tensor_copy(vs_picked[:], vs_win[:].indirect(offsets[:]))
-        vs_col = []
+        vs_col = keep.tile([P, B, 1, PACK], F32, name="vs_col")
         for b in range(B):
             turned = turn_bank()
             picked = vs_picked[:, b * N : (b + 1) * N].rearrange("p (m t) -> p t m", t=PACK)
             for t in range(PACK):
                 nc.tensor.transpose(turned[:, t, :], picked[:, t, :], ident[:])
-            c = keep.tile([P, 1, PACK], F32, name=f"vs_col{b}")
-            nc.scalar.copy(out=c[:], in_=turned[:, :, last:P].rearrange("p t o -> p o t"))
-            vs_col.append(c)
+            nc.scalar.copy(out=vs_col[:, b, :, :], in_=turned[:, :, last:P].rearrange("p t o -> p o t"))
 
         k_win = [keep.tile([P, T], U32, name=f"k_win{u}") for u in range(2)]
 
         def cast_pairs(u, lo, hi, share):
             pairs = k_win[u][:, lo:hi].bitcast(BF16).rearrange("p (t r) -> p t r", r=2)
-            rows = k_raw[u, lo][:].rearrange("p r t -> p t r")
+            rows = k_raw[u][:, :, lo:hi].rearrange("p r t -> p t r")
             nc.scalar.activation(pairs[:, 0:share, :], rows[:, 0:share, :], COPY)
             nc.vector.tensor_copy(pairs[:, share:, :], rows[:, share:, :])
 
@@ -96,31 +94,32 @@ def tile_attend_x_sigmoid_gate_kernel(tc, qT, kT, vT, vs, og, offs, out):
             for b in range(B):
                 nc.vector.tensor_copy(k_both[b][:, u, :].rearrange("p (t m) -> p m t", t=PACK), listed(k_win[u], b))
 
-        cast_pairs(0, 0, 1024, 768)
+        cast_pairs(0, 0, 1024, 352)
         cast_pairs(0, 1024, T, 352)
         gather_k(0)
         for lo, hi in key_chunks[1]:
             cast_pairs(1, lo, hi, (hi - lo) * 11 // 32)
         gather_k(1)
-        k_grouped = [
-            keep.tile([P, PACK * N], BF16, name=f"k_grouped{b}", tag=f"k_grouped{b}", align_bytes=64) for b in range(B)
-        ]
+        k_grouped = keep.tile([P, B, PACK * N], BF16, name="k_grouped", align_bytes=64)
         for b in range(B):
             nc.vector.tensor_copy(
-                k_grouped[b][:].bitcast(I32).rearrange("p (c u) -> p c u", u=2),
+                k_grouped[:, b, :].bitcast(I32).rearrange("p (c u) -> p c u", u=2),
                 k_both[b][:].bitcast(I32).rearrange("p u c -> p c u"),
             )
 
         q_grouped = keep.tile([P, B, NQ, PACK], BF16, name="q_grouped", align_bytes=64)
         q_codes = keep.tile([P, B * NQ], U32, name="q_codes", align_bytes=64)
         q_scales = keep.tile([P, B * NQ], U8, name="q_scales", align_bytes=64)
-        nc.scalar.copy(out=q_grouped[:], in_=q_raw[:].rearrange("p b (j q) -> p b q j", j=PACK))
+        nc.scalar.copy(
+            out=q_grouped[:].rearrange("p b (c i) j -> p b c j i", i=4),
+            in_=q_raw[:].rearrange("p b (j c i) -> p b c j i", j=PACK, i=4),
+        )
 
-        k_codes = [keep.tile([P, N], U32, name=f"k_codes{b}", align_bytes=64) for b in range(B)]
-        k_scales = [keep.tile([P, N], U8, name=f"k_scales{b}", align_bytes=64) for b in range(B)]
-        for b in range(B):
-            quantize(k_codes[b][:], k_scales[b][:], k_grouped[b][:])
+        k_codes = keep.tile([P, B * N], U32, name="k_codes", align_bytes=64)
+        k_scales = keep.tile([P, B * N], U8, name="k_scales", align_bytes=64)
         quantize(q_codes[:], q_scales[:], q_grouped[:].rearrange("p b q j -> p (b q j)"))
+        for b in range(B):
+            quantize(k_codes[:, b * N : (b + 1) * N], k_scales[:, b * N : (b + 1) * N], k_grouped[:, b, :])
 
         v0_win = keep.tile([P, T], BF16, name="v0_win")
         for c in range(2):
@@ -136,11 +135,11 @@ def tile_attend_x_sigmoid_gate_kernel(tc, qT, kT, vT, vs, og, offs, out):
         for b in range(B):
             bank = psum.tile([P, PACK, NQ], F32, name=f"score{b}")
             for t in range(PACK):
-                c = slice(t * P, (t + 1) * P)
+                c = slice(b * N + t * P, b * N + (t + 1) * P)
                 nc.tensor.matmul_mx(
                     out=bank[:, t, :],
-                    lhsT=k_codes[b][:, c].bitcast(FP8X4),
-                    lhsT_scale=k_scales[b][:, c],
+                    lhsT=k_codes[:, c].bitcast(FP8X4),
+                    lhsT_scale=k_scales[:, c],
                     rhs=q_codes[:, b * NQ : (b + 1) * NQ].bitcast(FP8X4),
                     rhs_scale=q_scales[:, b * NQ : (b + 1) * NQ],
                     start=True,
@@ -154,18 +153,17 @@ def tile_attend_x_sigmoid_gate_kernel(tc, qT, kT, vT, vs, og, offs, out):
             for u in range(2):
                 nc.tensor.transpose(bank[:, u, :], words[:, u * P : (u + 1) * P], ident[:])
 
-        v1_picked = [keep.tile([P, N], BF16, name=f"v1_picked{b}", tag=f"v1_picked{b}", align_bytes=64) for b in range(B)]
-        v1_grouped = []
-        for b in range(B):
-            nc.vector.tensor_copy(paired(v1_picked[b]), listed(v1_win, b))
-            bank = turn_bank()
-            turn_v(v1_picked[b][:].bitcast(F32), bank[:, 0:2, :])
-            g = keep.tile([P, P * PACK], BF16, name=f"v1_grouped{b}", align_bytes=64)
-            nc.scalar.copy(
-                out=g[:].bitcast(F32).rearrange("p (e u) -> p e u", u=2),
-                in_=bank[:, 0:2, :].rearrange("p u e -> p e u"),
-            )
-            v1_grouped.append(g)
+        v1_picked = keep.tile([P, B * N], BF16, name="v1_picked", tag="v1_picked", align_bytes=64)
+        nc.vector.tensor_copy(paired(v1_picked), v1_win[:].indirect(offsets[:]))
+        bank1 = turn_bank()
+        v1_words = v1_picked[:].bitcast(F32)
+        for c in range(PACK):
+            nc.tensor.transpose(bank1[:, c, :], v1_words[:, c * P : (c + 1) * P], ident[:])
+        v1_grouped = keep.tile([P, B * P * PACK], BF16, name="v1_grouped", align_bytes=64)
+        nc.scalar.copy(
+            out=v1_grouped[:].bitcast(F32).rearrange("p (b e u) -> p b e u", b=B, u=2),
+            in_=bank1[:].rearrange("p (u b) e -> p b e u", u=2),
+        )
 
         bank0 = turn_bank()
         for b in range(B):
@@ -176,24 +174,21 @@ def tile_attend_x_sigmoid_gate_kernel(tc, qT, kT, vT, vs, og, offs, out):
             in_=bank0[:].rearrange("p (b u) e -> p b e u", u=2),
         )
 
-        w_codes = [keep.tile([P, NQ], U32, name=f"w_codes{b}", align_bytes=64) for b in range(B)]
-        w_scales = [keep.tile([P, NQ], U8, name=f"w_scales{b}", align_bytes=64) for b in range(B)]
-        w_grouped = [
-            keep.tile([P, NQ, PACK], BF16, name=f"w_grouped{b}", tag=f"v1_picked{b}", align_bytes=64) for b in range(B)
-        ]
-        for b in range(B):
-            nc.vector.tensor_tensor(w_grouped[b][:], p_sb[:, b, :, :], vs_col[b][:].to_broadcast([P, NQ, PACK]), MULT)
-        for b in range(B):
-            quantize(w_codes[b][:], w_scales[b][:], w_grouped[b][:].rearrange("p q j -> p (q j)"))
+        w_codes = keep.tile([P, B * NQ], U32, name="w_codes", align_bytes=64)
+        w_scales = keep.tile([P, B * NQ], U8, name="w_scales", align_bytes=64)
+        w_grouped = keep.tile([P, B, NQ, PACK], BF16, name="w_grouped", tag="v1_win", align_bytes=64)
+        nc.vector.tensor_tensor(w_grouped[:], p_sb[:], vs_col[:].to_broadcast([P, B, NQ, PACK]), MULT)
+        quantize(w_codes[:], w_scales[:], w_grouped[:].rearrange("p b q j -> p (b q j)"))
 
         gate = keep.tile([P, B, DV], F32, name="gate", tag="v0_picked1")
-        nc.scalar.activation(gate[:], og_sb[:], SIGMOID)
+        for h in (1, 0):
+            nc.scalar.activation(gate[:, :, h * P : (h + 1) * P], og_sb[:, :, h * P : (h + 1) * P], SIGMOID)
 
         def weigh(y, b, codes, scales):
             nc.tensor.matmul_mx(
                 out=y,
-                lhsT=w_codes[b][:].bitcast(FP8X4),
-                lhsT_scale=w_scales[b][:],
+                lhsT=w_codes[:, b * NQ : (b + 1) * NQ].bitcast(FP8X4),
+                lhsT_scale=w_scales[:, b * NQ : (b + 1) * NQ],
                 rhs=codes.bitcast(FP8X4),
                 rhs_scale=scales,
                 start=True,
@@ -201,22 +196,13 @@ def tile_attend_x_sigmoid_gate_kernel(tc, qT, kT, vT, vs, og, offs, out):
             )
 
         out_q = out.rearrange("b q e -> q b e")
-        for b in range(B):
-            codes = keep.tile([P, P], U32, name=f"v1_codes{b}", align_bytes=64)
-            scales = keep.tile([P, P], U8, name=f"v1_scales{b}", align_bytes=64)
-            quantize(codes[:], scales[:], v1_grouped[b][:])
-            y1 = psum.tile([P, P], F32, name=f"y1{b}")
-            weigh(y1[:], b, codes[:], scales[:])
-            o1 = keep.tile([P, P], F32, name=f"o1{b}")
-            nc.vector.scalar_tensor_tensor(o1[:], y1[:], 1.0 / 16.0, gate[:, b, P:DV], MULT, MULT)
-            nc.sync.dma_start(out[b, :, P:DV], o1[:])
-
-        v0_codes = keep.tile([P, B * P], U32, name="v0_codes", align_bytes=64)
-        v0_scales = keep.tile([P, B * P], U8, name="v0_scales", align_bytes=64)
-        quantize(v0_codes[:], v0_scales[:], v0_grouped[:])
-        y0 = psum.tile([P, B, P], F32, name="y0")
-        for b in range(B):
-            weigh(y0[:, b, :], b, v0_codes[:, b * P : (b + 1) * P], v0_scales[:, b * P : (b + 1) * P])
-        o0 = keep.tile([P, B, P], F32, name="o0")
-        nc.vector.scalar_tensor_tensor(o0[:], y0[:], 1.0 / 16.0, gate[:, :, 0:P], MULT, MULT)
-        nc.sync.dma_start(out_q[:, :, 0:P], o0[:])
+        for h, grouped in ((1, v1_grouped), (0, v0_grouped)):
+            codes = keep.tile([P, B * P], U32, name=f"v_codes{h}", align_bytes=64)
+            scales = keep.tile([P, B * P], U8, name=f"v_scales{h}", align_bytes=64)
+            quantize(codes[:], scales[:], grouped[:])
+            y = psum.tile([P, B, P], F32, name=f"y{h}")
+            for b in range(B):
+                weigh(y[:, b, :], b, codes[:, b * P : (b + 1) * P], scales[:, b * P : (b + 1) * P])
+            o = keep.tile([P, B, P], F32, name=f"o{h}")
+            nc.vector.scalar_tensor_tensor(o[:], y[:], 1.0 / 16.0, gate[:, :, h * P : (h + 1) * P], MULT, MULT)
+            nc.sync.dma_start(out_q[:, :, h * P : (h + 1) * P], o[:])

@@ -50,7 +50,7 @@ def tile_attend_x_sigmoid_gate_kernel(tc, qT, kT, vT, vs, og, offs, out):
         v0_raw = [keep.tile([P, T // 2], F32, name=f"v0_raw{c}", tag=f"v0_raw{c}") for c in range(2)]
         for c in range(2):
             nc.sync.dma_start(v0_raw[c][:], vT[0:P, c * T // 2 : (c + 1) * T // 2])
-        v1_win = keep.tile([P, T], F32, name="v1_win", tag="v1_win", align_bytes=64)
+        v1_win = keep.tile([P, T], F32, name="v1_win")
         nc.sync.dma_start(v1_win[:], vT[P:DV, :])
         og_sb = keep.tile([P, B, DV], F32, name="og_sb")
         nc.sync.dma_start(og_sb[:], og.rearrange("b q e -> q b e"))
@@ -153,16 +153,15 @@ def tile_attend_x_sigmoid_gate_kernel(tc, qT, kT, vT, vs, og, offs, out):
             for u in range(2):
                 nc.tensor.transpose(bank[:, u, :], words[:, u * P : (u + 1) * P], ident[:])
 
-        v1_picked = keep.tile([P, B * N], BF16, name="v1_picked", tag="v1_picked", align_bytes=64)
-        nc.vector.tensor_copy(paired(v1_picked), v1_win[:].indirect(offsets[:]))
+        v1_picked = [keep.tile([P, N], BF16, name=f"v1_picked{b}", tag=f"v1_picked{b}", align_bytes=64) for b in range(B)]
         bank1 = turn_bank()
-        v1_words = v1_picked[:].bitcast(F32)
-        for c in range(PACK):
-            nc.tensor.transpose(bank1[:, c, :], v1_words[:, c * P : (c + 1) * P], ident[:])
+        for b in range(B):
+            nc.vector.tensor_copy(paired(v1_picked[b]), listed(v1_win, b))
+            turn_v(v1_picked[b][:].bitcast(F32), bank1[:, 2 * b : 2 * b + 2, :])
         v1_grouped = keep.tile([P, B * P * PACK], BF16, name="v1_grouped", align_bytes=64)
         nc.scalar.copy(
             out=v1_grouped[:].bitcast(F32).rearrange("p (b e u) -> p b e u", b=B, u=2),
-            in_=bank1[:].rearrange("p (u b) e -> p b e u", u=2),
+            in_=bank1[:].rearrange("p (b u) e -> p b e u", u=2),
         )
 
         bank0 = turn_bank()
@@ -176,9 +175,17 @@ def tile_attend_x_sigmoid_gate_kernel(tc, qT, kT, vT, vs, og, offs, out):
 
         w_codes = keep.tile([P, B * NQ], U32, name="w_codes", align_bytes=64)
         w_scales = keep.tile([P, B * NQ], U8, name="w_scales", align_bytes=64)
-        w_grouped = keep.tile([P, B, NQ, PACK], BF16, name="w_grouped", tag="v1_win", align_bytes=64)
-        nc.vector.tensor_tensor(w_grouped[:], p_sb[:], vs_col[:].to_broadcast([P, B, NQ, PACK]), MULT)
-        quantize(w_codes[:], w_scales[:], w_grouped[:].rearrange("p b q j -> p (b q j)"))
+        w_grouped = keep.tile([P, B, NQ, PACK], BF16, name="w_grouped", tag="v1_picked0", align_bytes=64)
+        for b in range(B):
+            nc.vector.tensor_tensor(
+                w_grouped[:, b, :, :], p_sb[:, b, :, :], vs_col[:, b, :, :].to_broadcast([P, NQ, PACK]), MULT
+            )
+        v_codes = [keep.tile([P, B * P], U32, name=f"v_codes{h}", align_bytes=64) for h in range(2)]
+        v_scales = [keep.tile([P, B * P], U8, name=f"v_scales{h}", align_bytes=64) for h in range(2)]
+        for b, (h, grouped) in enumerate(((1, v1_grouped), (0, v0_grouped))):
+            rows = slice(b * NQ, (b + 1) * NQ)
+            quantize(w_codes[:, rows], w_scales[:, rows], w_grouped[:, b, :, :].rearrange("p q j -> p (q j)"))
+            quantize(v_codes[h][:], v_scales[h][:], grouped[:])
 
         gate = keep.tile([P, B, DV], F32, name="gate", tag="v0_picked1")
         for h in (1, 0):
@@ -196,10 +203,8 @@ def tile_attend_x_sigmoid_gate_kernel(tc, qT, kT, vT, vs, og, offs, out):
             )
 
         out_q = out.rearrange("b q e -> q b e")
-        for h, grouped in ((1, v1_grouped), (0, v0_grouped)):
-            codes = keep.tile([P, B * P], U32, name=f"v_codes{h}", align_bytes=64)
-            scales = keep.tile([P, B * P], U8, name=f"v_scales{h}", align_bytes=64)
-            quantize(codes[:], scales[:], grouped[:])
+        for h in (1, 0):
+            codes, scales = v_codes[h], v_scales[h]
             y = psum.tile([P, B, P], F32, name=f"y{h}")
             for b in range(B):
                 weigh(y[:, b, :], b, codes[:, b * P : (b + 1) * P], scales[:, b * P : (b + 1) * P])

@@ -39,18 +39,18 @@ def tile_attend_x_sigmoid_gate_kernel(tc, qT, kT, vT, vs, og, offs, out):
         nc.vector.memset(vs_win[0:last, 0 : T // 2], 0.0)
 
         k_rows = kT.rearrange("(p j) t -> p j t", j=PACK)
-        key_chunks = [[(0, 1024), (1024, T)], [(0, 1024), (1024, 1536), (1536, T)]]
-        k_raw = [keep.tile([P, 2, T], F32, name=f"k_raw{u}") for u in range(2)]
+        key_chunks = [[(0, 1024, 768), (1024, T, 352)], [(0, 1024, 768), (1024, 1792, 288), (1792, T, 96)]]
+        k_raw = {}
         for u in range(2):
-            nc.sync.dma_start(k_raw[u][:, 0, :], k_rows[:, 2 * u, :])
-            for lo, hi in key_chunks[u]:
-                nc.sync.dma_start(k_raw[u][:, 1, lo:hi], k_rows[:, 2 * u + 1, lo:hi])
+            for lo, hi, share in key_chunks[u]:
+                k_raw[u, lo] = keep.tile([P, 2, hi - lo], F32, name=f"k_raw{u}_{lo}")
+                nc.sync.dma_start(k_raw[u, lo][:], k_rows[:, 2 * u : 2 * u + 2, lo:hi])
         q_raw = keep.tile([P, B, PACK * NQ], F32, name="q_raw")
         nc.sync.dma_start(q_raw[:], qT.rearrange("b (p j) q -> p b (j q)", j=PACK))
         v0_raw = [keep.tile([P, T // 2], F32, name=f"v0_raw{c}", tag=f"v0_raw{c}") for c in range(2)]
         for c in range(2):
             nc.sync.dma_start(v0_raw[c][:], vT[0:P, c * T // 2 : (c + 1) * T // 2])
-        v1_win = keep.tile([P, T], F32, name="v1_win")
+        v1_win = keep.tile([P, T], F32, name="v1_win", tag="v1_win", align_bytes=64)
         nc.sync.dma_start(v1_win[:], vT[P:DV, :])
         og_sb = keep.tile([P, B, DV], F32, name="og_sb")
         nc.sync.dma_start(og_sb[:], og.rearrange("b q e -> q b e"))
@@ -84,7 +84,7 @@ def tile_attend_x_sigmoid_gate_kernel(tc, qT, kT, vT, vs, og, offs, out):
 
         def cast_pairs(u, lo, hi, share):
             pairs = k_win[u][:, lo:hi].bitcast(BF16).rearrange("p (t r) -> p t r", r=2)
-            rows = k_raw[u][:, :, lo:hi].rearrange("p r t -> p t r")
+            rows = k_raw[u, lo][:].rearrange("p r t -> p t r")
             nc.scalar.activation(pairs[:, 0:share, :], rows[:, 0:share, :], COPY)
             nc.vector.tensor_copy(pairs[:, share:, :], rows[:, share:, :])
 
@@ -94,12 +94,10 @@ def tile_attend_x_sigmoid_gate_kernel(tc, qT, kT, vT, vs, og, offs, out):
             for b in range(B):
                 nc.vector.tensor_copy(k_both[b][:, u, :].rearrange("p (t m) -> p m t", t=PACK), listed(k_win[u], b))
 
-        cast_pairs(0, 0, 1024, 352)
-        cast_pairs(0, 1024, T, 352)
-        gather_k(0)
-        for lo, hi in key_chunks[1]:
-            cast_pairs(1, lo, hi, (hi - lo) * 11 // 32)
-        gather_k(1)
+        for u in range(2):
+            for lo, hi, share in key_chunks[u]:
+                cast_pairs(u, lo, hi, share)
+            gather_k(u)
         k_grouped = keep.tile([P, B, PACK * N], BF16, name="k_grouped", align_bytes=64)
         for b in range(B):
             nc.vector.tensor_copy(
@@ -129,11 +127,11 @@ def tile_attend_x_sigmoid_gate_kernel(tc, qT, kT, vT, vs, og, offs, out):
             return picked[:].rearrange("p (u m r) -> p m u r", u=2, r=2)
 
         v0_picked = [keep.tile([P, N], BF16, name=f"v0_picked{b}", tag=f"v0_picked{b}") for b in range(B)]
-        nc.scalar.activation(paired(v0_picked[0]), listed(v0_win, 0), COPY)
 
         p_sb = keep.tile([P, B, NQ, PACK], F32, name="p_sb", tag="v0_raw1")
         for b in range(B):
-            bank = psum.tile([P, PACK, NQ], F32, name=f"score{b}")
+            nc.scalar.activation(paired(v0_picked[b]), listed(v0_win, b), COPY)
+            bank = psum.tile([P, PACK, NQ], F32, name=f"score{b}", tag=f"score{b}")
             for t in range(PACK):
                 c = slice(b * N + t * P, b * N + (t + 1) * P)
                 nc.tensor.matmul_mx(
@@ -147,11 +145,18 @@ def tile_attend_x_sigmoid_gate_kernel(tc, qT, kT, vT, vs, og, offs, out):
                 )
             nc.scalar.activation(p_sb[:, b, :, :], bank[:].rearrange("p t q -> p q t"), SIGMOID)
 
-        nc.scalar.activation(paired(v0_picked[1]), listed(v0_win, 1), COPY)
-
         def turn_v(words, bank):
             for u in range(2):
                 nc.tensor.transpose(bank[:, u, :], words[:, u * P : (u + 1) * P], ident[:])
+
+        bank0 = psum.tile([P, PACK, P], F32, name="bank0", tag="score0")
+        for b in range(B):
+            turn_v(v0_picked[b][:].bitcast(F32), bank0[:, 2 * b : 2 * b + 2, :])
+        v0_grouped = keep.tile([P, B * P * PACK], BF16, name="v0_grouped", align_bytes=64)
+        nc.scalar.copy(
+            out=v0_grouped[:].bitcast(F32).rearrange("p (b e u) -> p b e u", b=B, u=2),
+            in_=bank0[:].rearrange("p (b u) e -> p b e u", u=2),
+        )
 
         v1_picked = [keep.tile([P, N], BF16, name=f"v1_picked{b}", tag=f"v1_picked{b}", align_bytes=64) for b in range(B)]
         bank1 = turn_bank()
@@ -164,31 +169,22 @@ def tile_attend_x_sigmoid_gate_kernel(tc, qT, kT, vT, vs, og, offs, out):
             in_=bank1[:].rearrange("p (b u) e -> p b e u", u=2),
         )
 
-        bank0 = turn_bank()
-        for b in range(B):
-            turn_v(v0_picked[b][:].bitcast(F32), bank0[:, 2 * b : 2 * b + 2, :])
-        v0_grouped = keep.tile([P, B * P * PACK], BF16, name="v0_grouped", align_bytes=64)
-        nc.scalar.copy(
-            out=v0_grouped[:].bitcast(F32).rearrange("p (b e u) -> p b e u", b=B, u=2),
-            in_=bank0[:].rearrange("p (b u) e -> p b e u", u=2),
-        )
-
         w_codes = keep.tile([P, B * NQ], U32, name="w_codes", align_bytes=64)
         w_scales = keep.tile([P, B * NQ], U8, name="w_scales", align_bytes=64)
-        w_grouped = keep.tile([P, B, NQ, PACK], BF16, name="w_grouped", tag="v1_picked0", align_bytes=64)
+        w_grouped = keep.tile([P, B, NQ, PACK], BF16, name="w_grouped", tag="v1_win", align_bytes=64)
         for b in range(B):
             nc.vector.tensor_tensor(
                 w_grouped[:, b, :, :], p_sb[:, b, :, :], vs_col[:, b, :, :].to_broadcast([P, NQ, PACK]), MULT
             )
         v_codes = [keep.tile([P, B * P], U32, name=f"v_codes{h}", align_bytes=64) for h in range(2)]
         v_scales = [keep.tile([P, B * P], U8, name=f"v_scales{h}", align_bytes=64) for h in range(2)]
-        for b, (h, grouped) in enumerate(((1, v1_grouped), (0, v0_grouped))):
+        for b, grouped in enumerate((v0_grouped, v1_grouped)):
             rows = slice(b * NQ, (b + 1) * NQ)
             quantize(w_codes[:, rows], w_scales[:, rows], w_grouped[:, b, :, :].rearrange("p q j -> p (q j)"))
-            quantize(v_codes[h][:], v_scales[h][:], grouped[:])
+            quantize(v_codes[b][:], v_scales[b][:], grouped[:])
 
-        gate = keep.tile([P, B, DV], F32, name="gate", tag="v0_picked1")
-        for h in (1, 0):
+        gate = keep.tile([P, B, DV], F32, name="gate", tag="v1_picked1", align_bytes=64)
+        for h in range(2):
             nc.scalar.activation(gate[:, :, h * P : (h + 1) * P], og_sb[:, :, h * P : (h + 1) * P], SIGMOID)
 
         def weigh(y, b, codes, scales):
@@ -203,7 +199,7 @@ def tile_attend_x_sigmoid_gate_kernel(tc, qT, kT, vT, vs, og, offs, out):
             )
 
         out_q = out.rearrange("b q e -> q b e")
-        for h in (1, 0):
+        for h in range(2):
             codes, scales = v_codes[h], v_scales[h]
             y = psum.tile([P, B, P], F32, name=f"y{h}")
             for b in range(B):

@@ -32,19 +32,20 @@ def tile_attend_x_sigmoid_gate_kernel(tc, qT, kT, vT, vs, og, offs, out):
         psum = ctx.enter_context(tc.psum_pool(name="psum", bufs=1))
 
         offsets = keep.tile([P, B * N // 16], U16, name="offsets")
-        nc.sync.dma_start(offsets[:], offs)
         vs_win = keep.tile([P, T], F32, name="vs_win")
-        nc.sync.dma_start(vs_win[last:P, :], vs[0:1, :])
         nc.gpsimd.memset(vs_win[0:last, T // 2 : T], 0.0)
         nc.vector.memset(vs_win[0:last, 0 : T // 2], 0.0)
 
         k_rows = kT.rearrange("(p j) t -> p j t", j=PACK)
-        key_chunks = [[(0, 1024, 768), (1024, T, 352)], [(0, 1024, 768), (1024, 1792, 288), (1792, T, 96)]]
+        key_chunks = [[(0, 1024, 1024), (1024, T, 480)], [(0, 1024, 768), (1024, 1792, 288), (1792, T, 96)]]
         k_raw = {}
         for u in range(2):
             for lo, hi, share in key_chunks[u]:
                 k_raw[u, lo] = keep.tile([P, 2, hi - lo], F32, name=f"k_raw{u}_{lo}")
                 nc.sync.dma_start(k_raw[u, lo][:], k_rows[:, 2 * u : 2 * u + 2, lo:hi])
+                if (u, lo) == (0, 0):
+                    nc.sync.dma_start(offsets[:], offs)
+                    nc.sync.dma_start(vs_win[last:P, :], vs[0:1, :])
         q_raw = keep.tile([P, B, PACK * NQ], F32, name="q_raw")
         nc.sync.dma_start(q_raw[:], qT.rearrange("b (p j) q -> p b (j q)", j=PACK))
         v0_raw = [keep.tile([P, T // 2], F32, name=f"v0_raw{c}", tag=f"v0_raw{c}") for c in range(2)]
@@ -86,7 +87,8 @@ def tile_attend_x_sigmoid_gate_kernel(tc, qT, kT, vT, vs, og, offs, out):
             pairs = k_win[u][:, lo:hi].bitcast(BF16).rearrange("p (t r) -> p t r", r=2)
             rows = k_raw[u, lo][:].rearrange("p r t -> p t r")
             nc.scalar.activation(pairs[:, 0:share, :], rows[:, 0:share, :], COPY)
-            nc.vector.tensor_copy(pairs[:, share:, :], rows[:, share:, :])
+            if share < hi - lo:
+                nc.vector.tensor_copy(pairs[:, share:, :], rows[:, share:, :])
 
         k_both = [keep.tile([P, 2, N], U32, name=f"k_both{b}") for b in range(B)]
 
@@ -129,8 +131,14 @@ def tile_attend_x_sigmoid_gate_kernel(tc, qT, kT, vT, vs, og, offs, out):
         v0_picked = [keep.tile([P, N], BF16, name=f"v0_picked{b}", tag=f"v0_picked{b}") for b in range(B)]
 
         p_sb = keep.tile([P, B, NQ, PACK], F32, name="p_sb", tag="v0_raw1")
+
+        def gather_v0(b, lo, hi):
+            part = offsets[:, b * cols + lo // 16 : b * cols + hi // 16]
+            nc.scalar.activation(paired(v0_picked[b])[:, lo // PACK : hi // PACK], v0_win[:].indirect(part), COPY)
+
+        gather_v0(0, 0, N)
         for b in range(B):
-            nc.scalar.activation(paired(v0_picked[b]), listed(v0_win, b), COPY)
+            gather_v0(1, b * N // 2, (b + 1) * N // 2)
             bank = psum.tile([P, PACK, NQ], F32, name=f"score{b}", tag=f"score{b}")
             for t in range(PACK):
                 c = slice(b * N + t * P, b * N + (t + 1) * P)
@@ -171,7 +179,7 @@ def tile_attend_x_sigmoid_gate_kernel(tc, qT, kT, vT, vs, og, offs, out):
 
         w_codes = keep.tile([P, B * NQ], U32, name="w_codes", align_bytes=64)
         w_scales = keep.tile([P, B * NQ], U8, name="w_scales", align_bytes=64)
-        w_grouped = keep.tile([P, B, NQ, PACK], BF16, name="w_grouped", tag="v1_win", align_bytes=64)
+        w_grouped = keep.tile([P, B, NQ, PACK], BF16, name="w_grouped", align_bytes=64)
         for b in range(B):
             nc.vector.tensor_tensor(
                 w_grouped[:, b, :, :], p_sb[:, b, :, :], vs_col[:, b, :, :].to_broadcast([P, NQ, PACK]), MULT

@@ -33,11 +33,12 @@ def tile_attend_x_sigmoid_gate_kernel(tc, qT, kT, vT, vs, og, offs, out):
 
         offsets = keep.tile([P, B * N // 16], U16, name="offsets")
         vs_win = keep.tile([P, T], F32, name="vs_win")
+        nc.scalar.dma_start(vs_win[last:P, :], vs[0:1, :])
         nc.gpsimd.memset(vs_win[0:last, T // 2 : T], 0.0)
         nc.vector.memset(vs_win[0:last, 0 : T // 2], 0.0)
 
         k_rows = kT.rearrange("(p j) t -> p j t", j=PACK)
-        key_chunks = [[(0, 1024, 1024), (1024, T, 480)], [(0, 1024, 768), (1024, 1792, 288), (1792, T, 96)]]
+        key_chunks = [[(0, 1024, 1024), (1024, T, 480)], [(0, 1024, 768), (1024, T, 352)]]
         k_raw = {}
         for u in range(2):
             for lo, hi, share in key_chunks[u]:
@@ -45,7 +46,6 @@ def tile_attend_x_sigmoid_gate_kernel(tc, qT, kT, vT, vs, og, offs, out):
                 nc.sync.dma_start(k_raw[u, lo][:], k_rows[:, 2 * u : 2 * u + 2, lo:hi])
                 if (u, lo) == (0, 0):
                     nc.sync.dma_start(offsets[:], offs)
-                    nc.sync.dma_start(vs_win[last:P, :], vs[0:1, :])
         q_raw = keep.tile([P, B, PACK * NQ], F32, name="q_raw")
         nc.sync.dma_start(q_raw[:], qT.rearrange("b (p j) q -> p b (j q)", j=PACK))
         v0_raw = [keep.tile([P, T // 2], F32, name=f"v0_raw{c}", tag=f"v0_raw{c}") for c in range(2)]

@@ -37,15 +37,15 @@ def tile_attend_x_sigmoid_gate_kernel(tc, qT, kT, vT, vs, og, offs, out):
         nc.gpsimd.memset(vs_win[0:last, T // 2 : T], 0.0)
         nc.vector.memset(vs_win[0:last, 0 : T // 2], 0.0)
 
-        k_rows = kT.rearrange("(p j) t -> p j t", j=PACK)
-        key_chunks = [[(0, 1024, 1024), (1024, T, 480)], [(0, 1024, 768), (1024, T, 352)]]
-        k_raw = {}
+        nc.sync.dma_start(offsets[:], offs)
+        k_rows = kT.rearrange("(p j) t -> p (j t)", j=PACK)
+        key_chunks = [[(0, 1024, 352), (1024, T, 352)], [(0, 1024, 352), (1024, T, 352)]]
+        k_raw = [keep.tile([P, 2 * T], F32, name=f"k_raw{u}") for u in range(2)]
         for u in range(2):
+            start = 0
             for lo, hi, share in key_chunks[u]:
-                k_raw[u, lo] = keep.tile([P, 2, hi - lo], F32, name=f"k_raw{u}_{lo}")
-                nc.sync.dma_start(k_raw[u, lo][:], k_rows[:, 2 * u : 2 * u + 2, lo:hi])
-                if (u, lo) == (0, 0):
-                    nc.sync.dma_start(offsets[:], offs)
+                nc.sync.dma_start(k_raw[u][:, start : T + hi], k_rows[:, 2 * u * T + start : (2 * u + 1) * T + hi])
+                start = T + hi
         q_raw = keep.tile([P, B, PACK * NQ], F32, name="q_raw")
         nc.sync.dma_start(q_raw[:], qT.rearrange("b (p j) q -> p b (j q)", j=PACK))
         v0_raw = [keep.tile([P, T // 2], F32, name=f"v0_raw{c}", tag=f"v0_raw{c}") for c in range(2)]
@@ -85,7 +85,7 @@ def tile_attend_x_sigmoid_gate_kernel(tc, qT, kT, vT, vs, og, offs, out):
 
         def cast_pairs(u, lo, hi, share):
             pairs = k_win[u][:, lo:hi].bitcast(BF16).rearrange("p (t r) -> p t r", r=2)
-            rows = k_raw[u, lo][:].rearrange("p r t -> p t r")
+            rows = k_raw[u][:].rearrange("p (r t) -> p t r", r=2)[:, lo:hi, :]
             nc.scalar.activation(pairs[:, 0:share, :], rows[:, 0:share, :], COPY)
             if share < hi - lo:
                 nc.vector.tensor_copy(pairs[:, share:, :], rows[:, share:, :])

@@ -73,13 +73,16 @@ def tile_attend_x_sigmoid_gate_kernel(tc, qT, kT, vT, vs, og, offs, out):
 
         vs_picked = keep.tile([P, B * N], F32, name="vs_picked")
         nc.vector.tensor_copy(vs_picked[:], vs_win[:].indirect(offsets[:]))
-        vs_col = keep.tile([P, B, 1, PACK], F32, name="vs_col")
+        vs_wide = keep.tile([P, B, NQ, PACK], F32, name="vs_wide")
         for b in range(B):
             turned = turn_bank()
             picked = vs_picked[:, b * N : (b + 1) * N].rearrange("p (m t) -> p t m", t=PACK)
             for t in range(PACK):
                 nc.tensor.transpose(turned[:, t, :], picked[:, t, :], ident[:])
-            nc.scalar.copy(out=vs_col[:, b, :, :], in_=turned[:, :, last:P].rearrange("p t o -> p o t"))
+            nc.scalar.copy(
+                out=vs_wide[:, b, :, :],
+                in_=turned[:, :, last:P].rearrange("p t o -> p o t").to_broadcast([P, NQ, PACK]),
+            )
 
         k_win = [keep.tile([P, T], U32, name=f"k_win{u}") for u in range(2)]
 
@@ -166,32 +169,36 @@ def tile_attend_x_sigmoid_gate_kernel(tc, qT, kT, vT, vs, og, offs, out):
             in_=bank0[:].rearrange("p (b u) e -> p b e u", u=2),
         )
 
-        v1_picked = [keep.tile([P, N], BF16, name=f"v1_picked{b}", tag=f"v1_picked{b}", align_bytes=64) for b in range(B)]
-        bank1 = turn_bank()
+        v1_picked = keep.tile([P, B * N], BF16, name="v1_picked", tag="v1_picked", align_bytes=64)
+        nc.vector.tensor_copy(paired(v1_picked), v1_win[:].indirect(offsets[:]))
+        v1_words = v1_picked[:].bitcast(F32).rearrange("p (u b m) -> p b u m", u=2, b=B)
+        v1_grouped = [keep.tile([P, P * PACK], BF16, name=f"v1_grouped{b}", align_bytes=64) for b in range(B)]
         for b in range(B):
-            nc.vector.tensor_copy(paired(v1_picked[b]), listed(v1_win, b))
-            turn_v(v1_picked[b][:].bitcast(F32), bank1[:, 2 * b : 2 * b + 2, :])
-        v1_grouped = keep.tile([P, B * P * PACK], BF16, name="v1_grouped", align_bytes=64)
-        nc.scalar.copy(
-            out=v1_grouped[:].bitcast(F32).rearrange("p (b e u) -> p b e u", b=B, u=2),
-            in_=bank1[:].rearrange("p (b u) e -> p b e u", u=2),
-        )
+            bank1 = turn_bank()
+            for u in range(2):
+                nc.tensor.transpose(bank1[:, u, :], v1_words[:, b, u, :], ident[:])
+            nc.scalar.copy(
+                out=v1_grouped[b][:].bitcast(F32).rearrange("p (e u) -> p e u", u=2),
+                in_=bank1[:, 0:2, :].rearrange("p u e -> p e u"),
+            )
 
         w_codes = keep.tile([P, B * NQ], U32, name="w_codes", align_bytes=64)
         w_scales = keep.tile([P, B * NQ], U8, name="w_scales", align_bytes=64)
         w_grouped = keep.tile([P, B, NQ, PACK], BF16, name="w_grouped", align_bytes=64)
         for b in range(B):
-            nc.vector.tensor_tensor(
-                w_grouped[:, b, :, :], p_sb[:, b, :, :], vs_col[:, b, :, :].to_broadcast([P, NQ, PACK]), MULT
-            )
+            nc.vector.tensor_tensor(w_grouped[:, b, :, :], p_sb[:, b, :, :], vs_wide[:, b, :, :], MULT)
         v_codes = [keep.tile([P, B * P], U32, name=f"v_codes{h}", align_bytes=64) for h in range(2)]
         v_scales = [keep.tile([P, B * P], U8, name=f"v_scales{h}", align_bytes=64) for h in range(2)]
-        for b, grouped in enumerate((v0_grouped, v1_grouped)):
+        for b in range(B):
             rows = slice(b * NQ, (b + 1) * NQ)
             quantize(w_codes[:, rows], w_scales[:, rows], w_grouped[:, b, :, :].rearrange("p q j -> p (q j)"))
-            quantize(v_codes[b][:], v_scales[b][:], grouped[:])
+            if b == 0:
+                quantize(v_codes[0][:], v_scales[0][:], v0_grouped[:])
+        for b in range(B):
+            c = slice(b * P, (b + 1) * P)
+            quantize(v_codes[1][:, c], v_scales[1][:, c], v1_grouped[b][:])
 
-        gate = keep.tile([P, B, DV], F32, name="gate", tag="v1_picked1", align_bytes=64)
+        gate = keep.tile([P, B, DV], F32, name="gate", tag="v1_picked", align_bytes=64)
         for h in range(2):
             nc.scalar.activation(gate[:, :, h * P : (h + 1) * P], og_sb[:, :, h * P : (h + 1) * P], SIGMOID)
 
@@ -206,12 +213,16 @@ def tile_attend_x_sigmoid_gate_kernel(tc, qT, kT, vT, vs, og, offs, out):
                 stop=True,
             )
 
-        out_q = out.rearrange("b q e -> q b e")
-        for h in range(2):
-            codes, scales = v_codes[h], v_scales[h]
-            y = psum.tile([P, B, P], F32, name=f"y{h}")
-            for b in range(B):
-                weigh(y[:, b, :], b, codes[:, b * P : (b + 1) * P], scales[:, b * P : (b + 1) * P])
-            o = keep.tile([P, B, P], F32, name=f"o{h}")
-            nc.vector.scalar_tensor_tensor(o[:], y[:], 1.0 / 16.0, gate[:, :, h * P : (h + 1) * P], MULT, MULT)
-            nc.sync.dma_start(out_q[:, :, h * P : (h + 1) * P], o[:])
+        y0 = psum.tile([P, B, P], F32, name="y0")
+        for b in range(B):
+            weigh(y0[:, b, :], b, v_codes[0][:, b * P : (b + 1) * P], v_scales[0][:, b * P : (b + 1) * P])
+        y1 = [psum.tile([P, P], F32, name=f"y1_{b}") for b in range(B)]
+        for b in range(B):
+            weigh(y1[b][:], b, v_codes[1][:, b * P : (b + 1) * P], v_scales[1][:, b * P : (b + 1) * P])
+        o0 = keep.tile([P, B, P], F32, name="o0")
+        nc.vector.scalar_tensor_tensor(o0[:], y0[:], 1.0 / 16.0, gate[:, :, 0:P], MULT, MULT)
+        nc.sync.dma_start(out.rearrange("b q e -> q b e")[:, :, 0:P], o0[:])
+        for b in range(B):
+            o1 = keep.tile([P, P], F32, name=f"o1_{b}")
+            nc.vector.scalar_tensor_tensor(o1[:], y1[b][:], 1.0 / 16.0, gate[:, b, P:DV], MULT, MULT)
+            nc.sync.dma_start(out[b, :, P:DV], o1[:])

@@ -17,9 +17,13 @@ FP8X4 = mybir.dt.float8_e4m3fn_x4
 SIGMOID = mybir.ActivationFunctionType.Sigmoid
 COPY = mybir.ActivationFunctionType.Copy
 MULT = mybir.AluOpType.mult
+ADD = mybir.AluOpType.add
 
 FLOPS = 2 * B * NQ * N * (D + DV)
 BYTES = 4 * (B * D * NQ + D * T + DV * T + T + 2 * B * NQ * DV) + 2 * P * (B * N // 16)
+
+KEY_PIECES = [[(0, 1024, 384), (1024, T, 384)], [(0, 1024, 384), (1024, 1664, 240), (1664, T, 144)]]
+ON_VECTOR = 128
 
 
 def tile_attend_x_sigmoid_gate_kernel(tc, qT, kT, vT, vs, og, offs, out):
@@ -29,7 +33,11 @@ def tile_attend_x_sigmoid_gate_kernel(tc, qT, kT, vT, vs, og, offs, out):
 
     with ExitStack() as ctx:
         keep = ctx.enter_context(tc.tile_pool(name="keep", bufs=1))
+        shared = ctx.enter_context(tc.tile_pool(name="shared", bufs=1))
         psum = ctx.enter_context(tc.psum_pool(name="psum", bufs=1))
+
+        def placed(shape, dtype, name, kib):
+            return shared.tile(shape, dtype, name=name, offset=kib * 1024, align_bytes=64)
 
         offsets = keep.tile([P, B * N // 16], U16, name="offsets")
         vs_win = keep.tile([P, T], F32, name="vs_win")
@@ -39,20 +47,18 @@ def tile_attend_x_sigmoid_gate_kernel(tc, qT, kT, vT, vs, og, offs, out):
 
         nc.sync.dma_start(offsets[:], offs)
         k_rows = kT.rearrange("(p j) t -> p (j t)", j=PACK)
-        key_chunks = [[(0, 1024, 352), (1024, T, 352)], [(0, 1024, 352), (1024, T, 352)]]
         k_raw = [keep.tile([P, 2 * T], F32, name=f"k_raw{u}") for u in range(2)]
         for u in range(2):
             start = 0
-            for lo, hi, share in key_chunks[u]:
+            for lo, hi, share in KEY_PIECES[u]:
                 nc.sync.dma_start(k_raw[u][:, start : T + hi], k_rows[:, 2 * u * T + start : (2 * u + 1) * T + hi])
                 start = T + hi
-        q_raw = keep.tile([P, B, PACK * NQ], F32, name="q_raw")
-        nc.sync.dma_start(q_raw[:], qT.rearrange("b (p j) q -> p b (j q)", j=PACK))
-        v0_raw = [keep.tile([P, T // 2], F32, name=f"v0_raw{c}", tag=f"v0_raw{c}") for c in range(2)]
-        for c in range(2):
-            nc.sync.dma_start(v0_raw[c][:], vT[0:P, c * T // 2 : (c + 1) * T // 2])
-        v1_win = keep.tile([P, T], F32, name="v1_win", tag="v1_win", align_bytes=64)
-        nc.sync.dma_start(v1_win[:], vT[P:DV, :])
+        q_raw = [keep.tile([P, PACK * NQ], F32, name="q_raw0"), placed([P, PACK * NQ], F32, "q_raw1", 16)]
+        for b in range(B):
+            nc.sync.dma_start(q_raw[b][:], qT[b].rearrange("(p j) q -> p (j q)", j=PACK))
+        v_win = [placed([P, T], F32, f"v_win{h}", 8 * h) for h in range(2)]
+        for h in range(2):
+            nc.sync.dma_start(v_win[h][:], vT[h * P : (h + 1) * P, :])
         og_sb = keep.tile([P, B, DV], F32, name="og_sb")
         nc.sync.dma_start(og_sb[:], og.rearrange("b q e -> q b e"))
 
@@ -62,14 +68,14 @@ def tile_attend_x_sigmoid_gate_kernel(tc, qT, kT, vT, vs, og, offs, out):
         ident = keep.tile([P, P], F32, name="ident")
         make_identity(nc, ident[:])
 
-        def listed(window, b):
-            return window[:].indirect(offsets[:, b * cols : (b + 1) * cols])
+        def listed(window, b, lo=0, hi=N):
+            return window[:].indirect(offsets[:, b * cols + lo // 16 : b * cols + hi // 16])
 
         def quantize(codes, scales, grouped):
             nc.vector.quantize_mx(out=codes.bitcast(FP8X4), scales=scales, in_=grouped)
 
         def turn_bank():
-            return psum.tile([P, PACK, P], F32, name="turned", tag="turned", bufs=3)
+            return psum.tile([P, PACK, P], F32, name="turned", tag="turned", bufs=2)
 
         vs_picked = keep.tile([P, B * N], F32, name="vs_picked")
         nc.vector.tensor_copy(vs_picked[:], vs_win[:].indirect(offsets[:]))
@@ -85,120 +91,131 @@ def tile_attend_x_sigmoid_gate_kernel(tc, qT, kT, vT, vs, og, offs, out):
             )
 
         k_win = [keep.tile([P, T], U32, name=f"k_win{u}") for u in range(2)]
-
-        def cast_pairs(u, lo, hi, share):
-            pairs = k_win[u][:, lo:hi].bitcast(BF16).rearrange("p (t r) -> p t r", r=2)
-            rows = k_raw[u][:].rearrange("p (r t) -> p t r", r=2)[:, lo:hi, :]
-            nc.scalar.activation(pairs[:, 0:share, :], rows[:, 0:share, :], COPY)
-            if share < hi - lo:
-                nc.vector.tensor_copy(pairs[:, share:, :], rows[:, share:, :])
-
         k_both = [keep.tile([P, 2, N], U32, name=f"k_both{b}") for b in range(B)]
-
-        def gather_k(u):
+        for u in range(2):
+            for lo, hi, share in KEY_PIECES[u]:
+                pairs = k_win[u][:, lo:hi].bitcast(BF16).rearrange("p (t r) -> p t r", r=2)
+                rows = k_raw[u][:].rearrange("p (r t) -> p t r", r=2)[:, lo:hi, :]
+                nc.scalar.activation(pairs[:, 0:share, :], rows[:, 0:share, :], COPY)
+                nc.vector.tensor_copy(pairs[:, share:, :], rows[:, share:, :])
             for b in range(B):
                 nc.vector.tensor_copy(k_both[b][:, u, :].rearrange("p (t m) -> p m t", t=PACK), listed(k_win[u], b))
 
-        for u in range(2):
-            for lo, hi, share in key_chunks[u]:
-                cast_pairs(u, lo, hi, share)
-            gather_k(u)
-        k_grouped = keep.tile([P, B, PACK * N], BF16, name="k_grouped", align_bytes=64)
-        for b in range(B):
-            nc.vector.tensor_copy(
-                k_grouped[:, b, :].bitcast(I32).rearrange("p (c u) -> p c u", u=2),
-                k_both[b][:].bitcast(I32).rearrange("p u c -> p c u"),
-            )
-
         q_grouped = keep.tile([P, B, NQ, PACK], BF16, name="q_grouped", align_bytes=64)
+        for b in range(B):
+            nc.gpsimd.tensor_scalar(
+                q_grouped[:, b, :, :], q_raw[b][:].rearrange("p (j q) -> p q j", j=PACK), 1.0, 0.0, MULT, ADD
+            )
         q_codes = keep.tile([P, B * NQ], U32, name="q_codes", align_bytes=64)
         q_scales = keep.tile([P, B * NQ], U8, name="q_scales", align_bytes=64)
+        quantize(q_codes[:], q_scales[:], q_grouped[:].rearrange("p b q j -> p (b q j)"))
+
+        half = N // 2
+        k_grouped0 = keep.tile([P, PACK * N], BF16, name="k_grouped0", align_bytes=64)
+        k_grouped1 = [
+            placed([P, PACK * half], BF16, "k_grouped1a", 16),
+            keep.tile([P, PACK * half], BF16, name="k_grouped1b", align_bytes=64),
+        ]
         nc.scalar.copy(
-            out=q_grouped[:].rearrange("p b (c i) j -> p b c j i", i=4),
-            in_=q_raw[:].rearrange("p b (j c i) -> p b c j i", j=PACK, i=4),
+            out=k_grouped0[:].bitcast(U32).rearrange("p (c u) -> p c u", u=2),
+            in_=k_both[0][:].rearrange("p u c -> p c u"),
+        )
+        nc.vector.tensor_copy(
+            k_grouped1[0][:].bitcast(I32).rearrange("p (c u) -> p c u", u=2),
+            k_both[1][:, :, 0:half].bitcast(I32).rearrange("p u c -> p c u"),
+        )
+        nc.scalar.copy(
+            out=k_grouped1[1][:].bitcast(U32).rearrange("p (c u) -> p c u", u=2),
+            in_=k_both[1][:, :, half:N].rearrange("p u c -> p c u"),
         )
 
-        k_codes = keep.tile([P, B * N], U32, name="k_codes", align_bytes=64)
-        k_scales = keep.tile([P, B * N], U8, name="k_scales", align_bytes=64)
-        quantize(q_codes[:], q_scales[:], q_grouped[:].rearrange("p b q j -> p (b q j)"))
-        for b in range(B):
-            quantize(k_codes[:, b * N : (b + 1) * N], k_scales[:, b * N : (b + 1) * N], k_grouped[:, b, :])
-
-        v0_win = keep.tile([P, T], BF16, name="v0_win")
+        k_scales = [keep.tile([P, N], U8, name=f"k_scales{b}", align_bytes=64) for b in range(B)]
+        k_codes = [keep.tile([P, N], U32, name="k_codes0", align_bytes=64), placed([P, N], U32, "k_codes1", 28)]
+        quantize(k_codes[0][:], k_scales[0][:], k_grouped0[:])
         for c in range(2):
-            nc.scalar.activation(v0_win[:, c * T // 2 : (c + 1) * T // 2], v0_raw[c][:], COPY)
+            part = slice(c * half, (c + 1) * half)
+            quantize(k_codes[1][:, part], k_scales[1][:, part], k_grouped1[c][:])
 
-        def paired(picked):
-            return picked[:].rearrange("p (u m r) -> p m u r", u=2, r=2)
+        score = [psum.tile([P, PACK, NQ], F32, name=f"score{b}") for b in range(B)]
 
-        v0_picked = [keep.tile([P, N], BF16, name=f"v0_picked{b}", tag=f"v0_picked{b}") for b in range(B)]
-
-        p_sb = keep.tile([P, B, NQ, PACK], F32, name="p_sb", tag="v0_raw1")
-
-        def gather_v0(b, lo, hi):
-            part = offsets[:, b * cols + lo // 16 : b * cols + hi // 16]
-            nc.scalar.activation(paired(v0_picked[b])[:, lo // PACK : hi // PACK], v0_win[:].indirect(part), COPY)
-
-        gather_v0(0, 0, N)
-        for b in range(B):
-            gather_v0(1, b * N // 2, (b + 1) * N // 2)
-            bank = psum.tile([P, PACK, NQ], F32, name=f"score{b}", tag=f"score{b}")
+        def scores(b):
             for t in range(PACK):
-                c = slice(b * N + t * P, b * N + (t + 1) * P)
+                c = slice(t * P, (t + 1) * P)
                 nc.tensor.matmul_mx(
-                    out=bank[:, t, :],
-                    lhsT=k_codes[:, c].bitcast(FP8X4),
-                    lhsT_scale=k_scales[:, c],
+                    out=score[b][:, t, :],
+                    lhsT=k_codes[b][:, c].bitcast(FP8X4),
+                    lhsT_scale=k_scales[b][:, c],
                     rhs=q_codes[:, b * NQ : (b + 1) * NQ].bitcast(FP8X4),
                     rhs_scale=q_scales[:, b * NQ : (b + 1) * NQ],
                     start=True,
                     stop=True,
                 )
-            nc.scalar.activation(p_sb[:, b, :, :], bank[:].rearrange("p t q -> p q t"), SIGMOID)
 
-        def turn_v(words, bank):
+        def sigmoid(p_sb, b):
+            nc.scalar.activation(p_sb[:], score[b][:].rearrange("p t q -> p q t"), SIGMOID)
+
+        def paired(picked):
+            return picked[:].rearrange("p (u m r) -> p m u r", u=2, r=2)
+
+        def turn_in_order(bank, picked):
+            words = picked[:].bitcast(F32).rearrange("p (m u) -> p u m", u=2)
+            for u in range(2):
+                nc.tensor.transpose(bank[:, u, :], words[:, u, :], ident[:])
+
+        def turn_paired(bank, picked):
+            words = picked[:].bitcast(F32)
             for u in range(2):
                 nc.tensor.transpose(bank[:, u, :], words[:, u * P : (u + 1) * P], ident[:])
 
-        bank0 = psum.tile([P, PACK, P], F32, name="bank0", tag="score0")
+        scores(0)
+        v_picked = [
+            [keep.tile([P, N], BF16, name=f"v_picked0{b}") for b in range(B)],
+            [keep.tile([P, N], BF16, name="v_picked10"), placed([P, N], BF16, "v_picked11", 32)],
+        ]
+        nc.scalar.activation(v_picked[0][0][:, ON_VECTOR:N], listed(v_win[0], 0, ON_VECTOR, N), COPY)
+        nc.vector.tensor_copy(v_picked[0][0][:, 0:ON_VECTOR], listed(v_win[0], 0, 0, ON_VECTOR))
+        nc.vector.tensor_copy(paired(v_picked[0][1]), listed(v_win[0], 1))
+        scores(1)
+        p0 = keep.tile([P, NQ, PACK], F32, name="p0")
+        sigmoid(p0, 0)
+        bank0 = psum.tile([P, PACK, P], F32, name="bank0")
+        turn_paired(bank0[:, 2:4, :], v_picked[0][1])
+        turn_in_order(bank0[:, 0:2, :], v_picked[0][0])
+
+        bank1 = [turn_bank() for b in range(B)]
         for b in range(B):
-            turn_v(v0_picked[b][:].bitcast(F32), bank0[:, 2 * b : 2 * b + 2, :])
-        v0_grouped = keep.tile([P, B * P * PACK], BF16, name="v0_grouped", align_bytes=64)
+            nc.vector.tensor_copy(paired(v_picked[1][b]), listed(v_win[1], b))
+            turn_paired(bank1[b], v_picked[1][b])
+
+        p1 = keep.tile([P, NQ, PACK], F32, name="p1")
+        sigmoid(p1, 1)
+        w_grouped = [keep.tile([P, NQ, PACK], BF16, name=f"w_grouped{b}", align_bytes=64) for b in range(B)]
+        for b, p_sb in enumerate((p0, p1)):
+            nc.gpsimd.tensor_tensor(w_grouped[b][:], p_sb[:], vs_wide[:, b, :, :], MULT)
+
+        v0_grouped = placed([P, B * P * PACK], BF16, "v0_grouped", 28)
         nc.scalar.copy(
             out=v0_grouped[:].bitcast(F32).rearrange("p (b e u) -> p b e u", b=B, u=2),
             in_=bank0[:].rearrange("p (b u) e -> p b e u", u=2),
         )
-
-        v1_picked = keep.tile([P, B * N], BF16, name="v1_picked", tag="v1_picked", align_bytes=64)
-        nc.vector.tensor_copy(paired(v1_picked), v1_win[:].indirect(offsets[:]))
-        v1_words = v1_picked[:].bitcast(F32).rearrange("p (u b m) -> p b u m", u=2, b=B)
         v1_grouped = [keep.tile([P, P * PACK], BF16, name=f"v1_grouped{b}", align_bytes=64) for b in range(B)]
         for b in range(B):
-            bank1 = turn_bank()
-            for u in range(2):
-                nc.tensor.transpose(bank1[:, u, :], v1_words[:, b, u, :], ident[:])
             nc.scalar.copy(
                 out=v1_grouped[b][:].bitcast(F32).rearrange("p (e u) -> p e u", u=2),
-                in_=bank1[:, 0:2, :].rearrange("p u e -> p e u"),
+                in_=bank1[b][:, 0:2, :].rearrange("p u e -> p e u"),
             )
 
-        w_codes = keep.tile([P, B * NQ], U32, name="w_codes", align_bytes=64)
+        w_codes = placed([P, B * NQ], U32, "w_codes", 8)
         w_scales = keep.tile([P, B * NQ], U8, name="w_scales", align_bytes=64)
-        w_grouped = keep.tile([P, B, NQ, PACK], BF16, name="w_grouped", align_bytes=64)
-        for b in range(B):
-            nc.vector.tensor_tensor(w_grouped[:, b, :, :], p_sb[:, b, :, :], vs_wide[:, b, :, :], MULT)
-        v_codes = [keep.tile([P, B * P], U32, name=f"v_codes{h}", align_bytes=64) for h in range(2)]
+        v_codes = [placed([P, B * P], U32, "v_codes0", 10), keep.tile([P, B * P], U32, name="v_codes1", align_bytes=64)]
         v_scales = [keep.tile([P, B * P], U8, name=f"v_scales{h}", align_bytes=64) for h in range(2)]
-        for b in range(B):
-            rows = slice(b * NQ, (b + 1) * NQ)
-            quantize(w_codes[:, rows], w_scales[:, rows], w_grouped[:, b, :, :].rearrange("p q j -> p (q j)"))
-            if b == 0:
-                quantize(v_codes[0][:], v_scales[0][:], v0_grouped[:])
+        quantize(v_codes[0][:], v_scales[0][:], v0_grouped[:])
         for b in range(B):
             c = slice(b * P, (b + 1) * P)
+            quantize(w_codes[:, c], w_scales[:, c], w_grouped[b][:].rearrange("p q j -> p (q j)"))
             quantize(v_codes[1][:, c], v_scales[1][:, c], v1_grouped[b][:])
 
-        gate = keep.tile([P, B, DV], F32, name="gate", tag="v1_picked", align_bytes=64)
+        gate = placed([P, B, DV], F32, "gate", 32)
         for h in range(2):
             nc.scalar.activation(gate[:, :, h * P : (h + 1) * P], og_sb[:, :, h * P : (h + 1) * P], SIGMOID)
 

@@ -23,7 +23,7 @@ FLOPS = 2 * B * NQ * N * (D + DV)
 BYTES = 4 * (B * D * NQ + D * T + DV * T + T + 2 * B * NQ * DV) + 2 * P * (B * N // 16)
 
 KEY_PIECES = [[(0, 1024, 384), (1024, T, 384)], [(0, 1024, 384), (1024, 1664, 240), (1664, T, 144)]]
-ON_VECTOR = 128
+ON_VECTOR = [256, 224]
 
 
 def tile_attend_x_sigmoid_gate_kernel(tc, qT, kT, vT, vs, og, offs, out):
@@ -53,14 +53,15 @@ def tile_attend_x_sigmoid_gate_kernel(tc, qT, kT, vT, vs, og, offs, out):
             for lo, hi, share in KEY_PIECES[u]:
                 nc.sync.dma_start(k_raw[u][:, start : T + hi], k_rows[:, 2 * u * T + start : (2 * u + 1) * T + hi])
                 start = T + hi
-        q_raw = [keep.tile([P, PACK * NQ], F32, name="q_raw0"), placed([P, PACK * NQ], F32, "q_raw1", 16)]
+        q_raw = [keep.tile([P, PACK * NQ], F32, name=f"q_raw{b}") for b in range(B)]
         for b in range(B):
             nc.sync.dma_start(q_raw[b][:], qT[b].rearrange("(p j) q -> p (j q)", j=PACK))
         v_win = [placed([P, T], F32, f"v_win{h}", 8 * h) for h in range(2)]
         for h in range(2):
             nc.sync.dma_start(v_win[h][:], vT[h * P : (h + 1) * P, :])
-        og_sb = keep.tile([P, B, DV], F32, name="og_sb")
-        nc.sync.dma_start(og_sb[:], og.rearrange("b q e -> q b e"))
+        og_sb = [placed([P, B, P], F32, "og_sb0", 36), keep.tile([P, B, P], F32, name="og_sb1")]
+        for h in range(2):
+            nc.sync.dma_start(og_sb[h][:], og.rearrange("b q e -> q b e")[:, :, h * P : (h + 1) * P])
 
         warm = keep.tile([P, 1], F32, name="warm")
         nc.vector.memset(warm[:], 0.0)
@@ -91,52 +92,42 @@ def tile_attend_x_sigmoid_gate_kernel(tc, qT, kT, vT, vs, og, offs, out):
             )
 
         k_win = [keep.tile([P, T], U32, name=f"k_win{u}") for u in range(2)]
-        k_both = [keep.tile([P, 2, N], U32, name=f"k_both{b}") for b in range(B)]
+        half = N // 2
+        k_both = [placed([P, 2, N], U32, f"k_both{b}", 20 + 4 * b) for b in range(B)]
         for u in range(2):
             for lo, hi, share in KEY_PIECES[u]:
                 pairs = k_win[u][:, lo:hi].bitcast(BF16).rearrange("p (t r) -> p t r", r=2)
                 rows = k_raw[u][:].rearrange("p (r t) -> p t r", r=2)[:, lo:hi, :]
                 nc.scalar.activation(pairs[:, 0:share, :], rows[:, 0:share, :], COPY)
                 nc.vector.tensor_copy(pairs[:, share:, :], rows[:, share:, :])
+            step = half if u == 1 else N
             for b in range(B):
-                nc.vector.tensor_copy(k_both[b][:, u, :].rearrange("p (t m) -> p m t", t=PACK), listed(k_win[u], b))
+                dealt = k_both[b][:, u, :].rearrange("p (t m) -> p m t", t=PACK)
+                for lo in range(0, N, step):
+                    nc.vector.tensor_copy(dealt[:, lo // PACK : (lo + step) // PACK, :], listed(k_win[u], b, lo, lo + step))
 
         q_grouped = keep.tile([P, B, NQ, PACK], BF16, name="q_grouped", align_bytes=64)
         for b in range(B):
-            nc.gpsimd.tensor_scalar(
-                q_grouped[:, b, :, :], q_raw[b][:].rearrange("p (j q) -> p q j", j=PACK), 1.0, 0.0, MULT, ADD
-            )
-        q_codes = keep.tile([P, B * NQ], U32, name="q_codes", align_bytes=64)
+            rows = q_raw[b][:].rearrange("p (j q) -> p q j", j=PACK)
+            nc.gpsimd.tensor_scalar(q_grouped[:, b, :, :], rows, 1.0, 0.0, MULT, ADD)
+
+        k_grouped = [keep.tile([P, PACK * N], BF16, name=f"k_grouped{b}", align_bytes=64) for b in range(B)]
+        for b in range(B):
+            woven = k_grouped[b][:].bitcast(U32).rearrange("p (t m u) -> p t m u", t=PACK, u=2)
+            words = k_both[b][:].rearrange("p u (t m) -> p t m u", t=PACK)
+            for lo in range(0, P, P // 2):
+                nc.scalar.copy(out=woven[:, :, lo : lo + P // 2, :], in_=words[:, :, lo : lo + P // 2, :])
+
+        q_codes = [keep.tile([P, NQ], U32, name="q_codes0", align_bytes=64), placed([P, NQ], U32, "q_codes1", 20)]
         q_scales = keep.tile([P, B * NQ], U8, name="q_scales", align_bytes=64)
-        quantize(q_codes[:], q_scales[:], q_grouped[:].rearrange("p b q j -> p (b q j)"))
-
-        half = N // 2
-        k_grouped0 = keep.tile([P, PACK * N], BF16, name="k_grouped0", align_bytes=64)
-        k_grouped1 = [
-            placed([P, PACK * half], BF16, "k_grouped1a", 16),
-            keep.tile([P, PACK * half], BF16, name="k_grouped1b", align_bytes=64),
-        ]
-        nc.scalar.copy(
-            out=k_grouped0[:].bitcast(U32).rearrange("p (c u) -> p c u", u=2),
-            in_=k_both[0][:].rearrange("p u c -> p c u"),
-        )
-        nc.vector.tensor_copy(
-            k_grouped1[0][:].bitcast(I32).rearrange("p (c u) -> p c u", u=2),
-            k_both[1][:, :, 0:half].bitcast(I32).rearrange("p u c -> p c u"),
-        )
-        nc.scalar.copy(
-            out=k_grouped1[1][:].bitcast(U32).rearrange("p (c u) -> p c u", u=2),
-            in_=k_both[1][:, :, half:N].rearrange("p u c -> p c u"),
-        )
-
+        k_codes = [keep.tile([P, N], U32, name=f"k_codes{b}", align_bytes=64) for b in range(B)]
         k_scales = [keep.tile([P, N], U8, name=f"k_scales{b}", align_bytes=64) for b in range(B)]
-        k_codes = [keep.tile([P, N], U32, name="k_codes0", align_bytes=64), placed([P, N], U32, "k_codes1", 28)]
-        quantize(k_codes[0][:], k_scales[0][:], k_grouped0[:])
-        for c in range(2):
-            part = slice(c * half, (c + 1) * half)
-            quantize(k_codes[1][:, part], k_scales[1][:, part], k_grouped1[c][:])
+        for b in range(B):
+            c = slice(b * NQ, (b + 1) * NQ)
+            quantize(q_codes[b][:], q_scales[:, c], q_grouped[:, b, :, :].rearrange("p q j -> p (q j)"))
+            quantize(k_codes[b][:], k_scales[b][:], k_grouped[b][:])
 
-        score = [psum.tile([P, PACK, NQ], F32, name=f"score{b}") for b in range(B)]
+        score = [psum.tile([P, PACK, NQ], F32, name=f"score{b}", tag=f"score{b}") for b in range(B)]
 
         def scores(b):
             for t in range(PACK):
@@ -145,7 +136,7 @@ def tile_attend_x_sigmoid_gate_kernel(tc, qT, kT, vT, vs, og, offs, out):
                     out=score[b][:, t, :],
                     lhsT=k_codes[b][:, c].bitcast(FP8X4),
                     lhsT_scale=k_scales[b][:, c],
-                    rhs=q_codes[:, b * NQ : (b + 1) * NQ].bitcast(FP8X4),
+                    rhs=q_codes[b][:].bitcast(FP8X4),
                     rhs_scale=q_scales[:, b * NQ : (b + 1) * NQ],
                     start=True,
                     stop=True,
@@ -168,36 +159,42 @@ def tile_attend_x_sigmoid_gate_kernel(tc, qT, kT, vT, vs, og, offs, out):
                 nc.tensor.transpose(bank[:, u, :], words[:, u * P : (u + 1) * P], ident[:])
 
         scores(0)
+        scores(1)
         v_picked = [
-            [keep.tile([P, N], BF16, name=f"v_picked0{b}") for b in range(B)],
+            [placed([P, N], BF16, f"v_picked0{b}", 24 + b) for b in range(B)],
             [keep.tile([P, N], BF16, name="v_picked10"), placed([P, N], BF16, "v_picked11", 32)],
         ]
-        nc.scalar.activation(v_picked[0][0][:, ON_VECTOR:N], listed(v_win[0], 0, ON_VECTOR, N), COPY)
-        nc.vector.tensor_copy(v_picked[0][0][:, 0:ON_VECTOR], listed(v_win[0], 0, 0, ON_VECTOR))
-        nc.vector.tensor_copy(paired(v_picked[0][1]), listed(v_win[0], 1))
-        scores(1)
+
+        def gather_values(h):
+            cut = ON_VECTOR[h]
+            nc.scalar.activation(v_picked[h][0][:, cut:N], listed(v_win[h], 0, cut, N), COPY)
+            nc.vector.tensor_copy(v_picked[h][0][:, 0:cut], listed(v_win[h], 0, 0, cut))
+            nc.vector.tensor_copy(paired(v_picked[h][1]), listed(v_win[h], 1))
+
+        gather_values(0)
         p0 = keep.tile([P, NQ, PACK], F32, name="p0")
         sigmoid(p0, 0)
-        bank0 = psum.tile([P, PACK, P], F32, name="bank0")
-        turn_paired(bank0[:, 2:4, :], v_picked[0][1])
-        turn_in_order(bank0[:, 0:2, :], v_picked[0][0])
-
-        bank1 = [turn_bank() for b in range(B)]
-        for b in range(B):
-            nc.vector.tensor_copy(paired(v_picked[1][b]), listed(v_win[1], b))
-            turn_paired(bank1[b], v_picked[1][b])
-
         p1 = keep.tile([P, NQ, PACK], F32, name="p1")
         sigmoid(p1, 1)
+        bank0 = [psum.tile([P, 2, P], F32, name="bank00", tag="score0"), psum.tile([P, 2, P], F32, name="bank01")]
+        turn_in_order(bank0[0], v_picked[0][0])
+        turn_paired(bank0[1], v_picked[0][1])
+
+        gather_values(1)
+        bank1 = [turn_bank() for b in range(B)]
+        turn_in_order(bank1[0], v_picked[1][0])
+        turn_paired(bank1[1], v_picked[1][1])
+
         w_grouped = [keep.tile([P, NQ, PACK], BF16, name=f"w_grouped{b}", align_bytes=64) for b in range(B)]
         for b, p_sb in enumerate((p0, p1)):
             nc.gpsimd.tensor_tensor(w_grouped[b][:], p_sb[:], vs_wide[:, b, :, :], MULT)
 
-        v0_grouped = placed([P, B * P * PACK], BF16, "v0_grouped", 28)
-        nc.scalar.copy(
-            out=v0_grouped[:].bitcast(F32).rearrange("p (b e u) -> p b e u", b=B, u=2),
-            in_=bank0[:].rearrange("p (b u) e -> p b e u", u=2),
-        )
+        gate = [keep.tile([P, B, P], F32, name="gate0")]
+        nc.scalar.activation(gate[0][:], og_sb[0][:], SIGMOID)
+        v0_grouped = [placed([P, P * PACK], BF16, "v0_grouped0", 12), placed([P, P * PACK], BF16, "v0_grouped1", 36)]
+        v0_words = [v0_grouped[b][:].bitcast(F32).rearrange("p (e u) -> p e u", u=2) for b in range(B)]
+        nc.vector.tensor_copy(v0_words[0], bank0[0][:].rearrange("p u e -> p e u"))
+        nc.scalar.copy(out=v0_words[1], in_=bank0[1][:].rearrange("p u e -> p e u"))
         v1_grouped = [keep.tile([P, P * PACK], BF16, name=f"v1_grouped{b}", align_bytes=64) for b in range(B)]
         for b in range(B):
             nc.scalar.copy(
@@ -207,17 +204,18 @@ def tile_attend_x_sigmoid_gate_kernel(tc, qT, kT, vT, vs, og, offs, out):
 
         w_codes = placed([P, B * NQ], U32, "w_codes", 8)
         w_scales = keep.tile([P, B * NQ], U8, name="w_scales", align_bytes=64)
-        v_codes = [placed([P, B * P], U32, "v_codes0", 10), keep.tile([P, B * P], U32, name="v_codes1", align_bytes=64)]
+        v_codes = [keep.tile([P, B * P], U32, name=f"v_codes{h}", align_bytes=64) for h in range(2)]
         v_scales = [keep.tile([P, B * P], U8, name=f"v_scales{h}", align_bytes=64) for h in range(2)]
-        quantize(v_codes[0][:], v_scales[0][:], v0_grouped[:])
         for b in range(B):
             c = slice(b * P, (b + 1) * P)
             quantize(w_codes[:, c], w_scales[:, c], w_grouped[b][:].rearrange("p q j -> p (q j)"))
-            quantize(v_codes[1][:, c], v_scales[1][:, c], v1_grouped[b][:])
+        for h, grouped in enumerate((v0_grouped, v1_grouped)):
+            for b in range(B):
+                c = slice(b * P, (b + 1) * P)
+                quantize(v_codes[h][:, c], v_scales[h][:, c], grouped[b][:])
 
-        gate = placed([P, B, DV], F32, "gate", 32)
-        for h in range(2):
-            nc.scalar.activation(gate[:, :, h * P : (h + 1) * P], og_sb[:, :, h * P : (h + 1) * P], SIGMOID)
+        gate.append(placed([P, B, P], F32, "gate1", 32))
+        nc.scalar.activation(gate[1][:], og_sb[1][:], SIGMOID)
 
         def weigh(y, b, codes, scales):
             nc.tensor.matmul_mx(
@@ -237,9 +235,9 @@ def tile_attend_x_sigmoid_gate_kernel(tc, qT, kT, vT, vs, og, offs, out):
         for b in range(B):
             weigh(y1[b][:], b, v_codes[1][:, b * P : (b + 1) * P], v_scales[1][:, b * P : (b + 1) * P])
         o0 = keep.tile([P, B, P], F32, name="o0")
-        nc.vector.scalar_tensor_tensor(o0[:], y0[:], 1.0 / 16.0, gate[:, :, 0:P], MULT, MULT)
+        nc.vector.scalar_tensor_tensor(o0[:], y0[:], 1.0 / 16.0, gate[0][:], MULT, MULT)
         nc.sync.dma_start(out.rearrange("b q e -> q b e")[:, :, 0:P], o0[:])
         for b in range(B):
             o1 = keep.tile([P, P], F32, name=f"o1_{b}")
-            nc.vector.scalar_tensor_tensor(o1[:], y1[b][:], 1.0 / 16.0, gate[:, b, P:DV], MULT, MULT)
+            nc.vector.scalar_tensor_tensor(o1[:], y1[b][:], 1.0 / 16.0, gate[1][:, b, :], MULT, MULT)
             nc.sync.dma_start(out[b, :, P:DV], o1[:])

@@ -23,7 +23,7 @@ FLOPS = 2 * B * NQ * N * (D + DV)
 BYTES = 4 * (B * D * NQ + D * T + DV * T + T + 2 * B * NQ * DV) + 2 * P * (B * N // 16)
 
 KEY_PIECES = [[(0, 1024, 384), (1024, T, 384)], [(0, 1024, 384), (1024, 1664, 240), (1664, T, 144)]]
-ON_VECTOR = [256, 224]
+ON_VECTOR = 256
 
 
 def tile_attend_x_sigmoid_gate_kernel(tc, qT, kT, vT, vs, og, offs, out):
@@ -37,7 +37,7 @@ def tile_attend_x_sigmoid_gate_kernel(tc, qT, kT, vT, vs, og, offs, out):
         psum = ctx.enter_context(tc.psum_pool(name="psum", bufs=1))
 
         def placed(shape, dtype, name, kib):
-            return shared.tile(shape, dtype, name=name, offset=kib * 1024, align_bytes=64)
+            return shared.tile(shape, dtype, name=name, offset=int(kib * 1024), align_bytes=64)
 
         offsets = keep.tile([P, B * N // 16], U16, name="offsets")
         vs_win = keep.tile([P, T], F32, name="vs_win")
@@ -47,7 +47,7 @@ def tile_attend_x_sigmoid_gate_kernel(tc, qT, kT, vT, vs, og, offs, out):
 
         nc.sync.dma_start(offsets[:], offs)
         k_rows = kT.rearrange("(p j) t -> p (j t)", j=PACK)
-        k_raw = [keep.tile([P, 2 * T], F32, name=f"k_raw{u}") for u in range(2)]
+        k_raw = [keep.tile([P, 2 * T], F32, name="k_raw0"), placed([P, 2 * T], F32, "k_raw1", 40)]
         for u in range(2):
             start = 0
             for lo, hi, share in KEY_PIECES[u]:
@@ -59,9 +59,8 @@ def tile_attend_x_sigmoid_gate_kernel(tc, qT, kT, vT, vs, og, offs, out):
         v_win = [placed([P, T], F32, f"v_win{h}", 8 * h) for h in range(2)]
         for h in range(2):
             nc.sync.dma_start(v_win[h][:], vT[h * P : (h + 1) * P, :])
-        og_sb = [placed([P, B, P], F32, "og_sb0", 36), keep.tile([P, B, P], F32, name="og_sb1")]
-        for h in range(2):
-            nc.sync.dma_start(og_sb[h][:], og.rearrange("b q e -> q b e")[:, :, h * P : (h + 1) * P])
+        og_sb = keep.tile([P, B, DV], F32, name="og_sb")
+        nc.sync.dma_start(og_sb[:], og.rearrange("b q e -> q b e"))
 
         warm = keep.tile([P, 1], F32, name="warm")
         nc.vector.memset(warm[:], 0.0)
@@ -93,41 +92,59 @@ def tile_attend_x_sigmoid_gate_kernel(tc, qT, kT, vT, vs, og, offs, out):
 
         k_win = [keep.tile([P, T], U32, name=f"k_win{u}") for u in range(2)]
         half = N // 2
-        k_both = [placed([P, 2, N], U32, f"k_both{b}", 20 + 4 * b) for b in range(B)]
+        k_both = [placed([P, 2, N], U32, "k_both0", 20), keep.tile([P, 2, N], U32, name="k_both1")]
         for u in range(2):
             for lo, hi, share in KEY_PIECES[u]:
                 pairs = k_win[u][:, lo:hi].bitcast(BF16).rearrange("p (t r) -> p t r", r=2)
                 rows = k_raw[u][:].rearrange("p (r t) -> p t r", r=2)[:, lo:hi, :]
                 nc.scalar.activation(pairs[:, 0:share, :], rows[:, 0:share, :], COPY)
                 nc.vector.tensor_copy(pairs[:, share:, :], rows[:, share:, :])
-            step = half if u == 1 else N
             for b in range(B):
+                step = half if (u, b) == (1, 0) else N
                 dealt = k_both[b][:, u, :].rearrange("p (t m) -> p m t", t=PACK)
                 for lo in range(0, N, step):
                     nc.vector.tensor_copy(dealt[:, lo // PACK : (lo + step) // PACK, :], listed(k_win[u], b, lo, lo + step))
 
-        q_grouped = keep.tile([P, B, NQ, PACK], BF16, name="q_grouped", align_bytes=64)
+        q_grouped = placed([P, B, NQ, PACK], BF16, "q_grouped", 40)
         for b in range(B):
             rows = q_raw[b][:].rearrange("p (j q) -> p q j", j=PACK)
             nc.gpsimd.tensor_scalar(q_grouped[:, b, :, :], rows, 1.0, 0.0, MULT, ADD)
 
-        k_grouped = [keep.tile([P, PACK * N], BF16, name=f"k_grouped{b}", align_bytes=64) for b in range(B)]
-        for b in range(B):
-            woven = k_grouped[b][:].bitcast(U32).rearrange("p (t m u) -> p t m u", t=PACK, u=2)
-            words = k_both[b][:].rearrange("p u (t m) -> p t m u", t=PACK)
-            for lo in range(0, P, P // 2):
-                nc.scalar.copy(out=woven[:, :, lo : lo + P // 2, :], in_=words[:, :, lo : lo + P // 2, :])
+        k_grouped0 = keep.tile([P, PACK * N], BF16, name="k_grouped0", align_bytes=64)
+        woven = k_grouped0[:].bitcast(U32).rearrange("p (t m u) -> p t m u", t=PACK, u=2)
+        words = k_both[0][:].rearrange("p u (t m) -> p t m u", t=PACK)
+        for lo in range(0, P, P // 2):
+            nc.scalar.copy(out=woven[:, :, lo : lo + P // 2, :], in_=words[:, :, lo : lo + P // 2, :])
 
-        q_codes = [keep.tile([P, NQ], U32, name="q_codes0", align_bytes=64), placed([P, NQ], U32, "q_codes1", 20)]
+        q_codes = [keep.tile([P, NQ], U32, name="q_codes0", align_bytes=64), placed([P, NQ], U32, "q_codes1", 22)]
         q_scales = keep.tile([P, B * NQ], U8, name="q_scales", align_bytes=64)
-        k_codes = [keep.tile([P, N], U32, name=f"k_codes{b}", align_bytes=64) for b in range(B)]
+        k_codes = [keep.tile([P, N], U32, name="k_codes0", align_bytes=64), placed([P, N], U32, "k_codes1", 28)]
         k_scales = [keep.tile([P, N], U8, name=f"k_scales{b}", align_bytes=64) for b in range(B)]
-        for b in range(B):
+
+        def quantize_queries(b):
             c = slice(b * NQ, (b + 1) * NQ)
             quantize(q_codes[b][:], q_scales[:, c], q_grouped[:, b, :, :].rearrange("p q j -> p (q j)"))
-            quantize(k_codes[b][:], k_scales[b][:], k_grouped[b][:])
 
-        score = [psum.tile([P, PACK, NQ], F32, name=f"score{b}", tag=f"score{b}") for b in range(B)]
+        quantize_queries(0)
+        quantize(k_codes[0][:], k_scales[0][:], k_grouped0[:])
+        k_grouped1 = [
+            keep.tile([P, PACK * half], BF16, name="k_grouped1a", align_bytes=64),
+            placed([P, PACK * half], BF16, "k_grouped1b", 20),
+        ]
+        nc.scalar.copy(
+            out=k_grouped1[0][:].bitcast(U32).rearrange("p (c u) -> p c u", u=2),
+            in_=k_both[1][:, :, 0:half].rearrange("p u c -> p c u"),
+        )
+        nc.vector.tensor_copy(
+            k_grouped1[1][:].bitcast(I32).rearrange("p (c u) -> p c u", u=2),
+            k_both[1][:, :, half:N].bitcast(I32).rearrange("p u c -> p c u"),
+        )
+        quantize_queries(1)
+        for c in range(2):
+            part = slice(c * half, (c + 1) * half)
+            quantize(k_codes[1][:, part], k_scales[1][:, part], k_grouped1[c][:])
+
+        score = [psum.tile([P, PACK, NQ], F32, name=f"score{b}") for b in range(B)]
 
         def scores(b):
             for t in range(PACK):
@@ -160,42 +177,37 @@ def tile_attend_x_sigmoid_gate_kernel(tc, qT, kT, vT, vs, og, offs, out):
 
         scores(0)
         scores(1)
-        v_picked = [
-            [placed([P, N], BF16, f"v_picked0{b}", 24 + b) for b in range(B)],
-            [keep.tile([P, N], BF16, name="v_picked10"), placed([P, N], BF16, "v_picked11", 32)],
-        ]
+        v_picked = [[keep.tile([P, N], BF16, name=f"v_picked{h}{b}") for b in range(B)] for h in range(2)]
+        nc.scalar.activation(v_picked[0][0][:, ON_VECTOR:N], listed(v_win[0], 0, ON_VECTOR, N), COPY)
+        nc.vector.tensor_copy(v_picked[0][0][:, 0:ON_VECTOR], listed(v_win[0], 0, 0, ON_VECTOR))
+        nc.vector.tensor_copy(paired(v_picked[0][1]), listed(v_win[0], 1))
+        p_sb = [keep.tile([P, NQ, PACK], F32, name=f"p{b}") for b in range(B)]
+        for b in range(B):
+            sigmoid(p_sb[b], b)
+        bank0 = psum.tile([P, PACK, P], F32, name="bank0")
+        turn_in_order(bank0[:, 0:2, :], v_picked[0][0])
+        turn_paired(bank0[:, 2:4, :], v_picked[0][1])
 
-        def gather_values(h):
-            cut = ON_VECTOR[h]
-            nc.scalar.activation(v_picked[h][0][:, cut:N], listed(v_win[h], 0, cut, N), COPY)
-            nc.vector.tensor_copy(v_picked[h][0][:, 0:cut], listed(v_win[h], 0, 0, cut))
-            nc.vector.tensor_copy(paired(v_picked[h][1]), listed(v_win[h], 1))
-
-        gather_values(0)
-        p0 = keep.tile([P, NQ, PACK], F32, name="p0")
-        sigmoid(p0, 0)
-        p1 = keep.tile([P, NQ, PACK], F32, name="p1")
-        sigmoid(p1, 1)
-        bank0 = [psum.tile([P, 2, P], F32, name="bank00", tag="score0"), psum.tile([P, 2, P], F32, name="bank01")]
-        turn_in_order(bank0[0], v_picked[0][0])
-        turn_paired(bank0[1], v_picked[0][1])
-
-        gather_values(1)
         bank1 = [turn_bank() for b in range(B)]
-        turn_in_order(bank1[0], v_picked[1][0])
-        turn_paired(bank1[1], v_picked[1][1])
+        for b in range(B):
+            nc.vector.tensor_copy(paired(v_picked[1][b]), listed(v_win[1], b))
+            turn_paired(bank1[b], v_picked[1][b])
 
         w_grouped = [keep.tile([P, NQ, PACK], BF16, name=f"w_grouped{b}", align_bytes=64) for b in range(B)]
-        for b, p_sb in enumerate((p0, p1)):
-            nc.gpsimd.tensor_tensor(w_grouped[b][:], p_sb[:], vs_wide[:, b, :, :], MULT)
+        for b in range(B):
+            nc.gpsimd.tensor_tensor(w_grouped[b][:], p_sb[b][:], vs_wide[:, b, :, :], MULT)
 
-        gate = [keep.tile([P, B, P], F32, name="gate0")]
-        nc.scalar.activation(gate[0][:], og_sb[0][:], SIGMOID)
-        v0_grouped = [placed([P, P * PACK], BF16, "v0_grouped0", 12), placed([P, P * PACK], BF16, "v0_grouped1", 36)]
-        v0_words = [v0_grouped[b][:].bitcast(F32).rearrange("p (e u) -> p e u", u=2) for b in range(B)]
-        nc.vector.tensor_copy(v0_words[0], bank0[0][:].rearrange("p u e -> p e u"))
-        nc.scalar.copy(out=v0_words[1], in_=bank0[1][:].rearrange("p u e -> p e u"))
-        v1_grouped = [keep.tile([P, P * PACK], BF16, name=f"v1_grouped{b}", align_bytes=64) for b in range(B)]
+        v0_grouped = placed([P, B * P * PACK], BF16, "v0_grouped", 28)
+        nc.scalar.copy(
+            out=v0_grouped[:].bitcast(F32).rearrange("p (b e u) -> p b e u", b=B, u=2),
+            in_=bank0[:].rearrange("p (b u) e -> p b e u", u=2),
+        )
+        gate = keep.tile([P, B, DV], F32, name="gate")
+        nc.scalar.activation(gate[:], og_sb[:], SIGMOID)
+        v1_grouped = [
+            keep.tile([P, P * PACK], BF16, name="v1_grouped0", align_bytes=64),
+            placed([P, P * PACK], BF16, "v1_grouped1", 32),
+        ]
         for b in range(B):
             nc.scalar.copy(
                 out=v1_grouped[b][:].bitcast(F32).rearrange("p (e u) -> p e u", u=2),
@@ -204,18 +216,13 @@ def tile_attend_x_sigmoid_gate_kernel(tc, qT, kT, vT, vs, og, offs, out):
 
         w_codes = placed([P, B * NQ], U32, "w_codes", 8)
         w_scales = keep.tile([P, B * NQ], U8, name="w_scales", align_bytes=64)
-        v_codes = [keep.tile([P, B * P], U32, name=f"v_codes{h}", align_bytes=64) for h in range(2)]
+        v_codes = [placed([P, B * P], U32, "v_codes0", 10), keep.tile([P, B * P], U32, name="v_codes1", align_bytes=64)]
         v_scales = [keep.tile([P, B * P], U8, name=f"v_scales{h}", align_bytes=64) for h in range(2)]
+        quantize(v_codes[0][:], v_scales[0][:], v0_grouped[:])
         for b in range(B):
             c = slice(b * P, (b + 1) * P)
             quantize(w_codes[:, c], w_scales[:, c], w_grouped[b][:].rearrange("p q j -> p (q j)"))
-        for h, grouped in enumerate((v0_grouped, v1_grouped)):
-            for b in range(B):
-                c = slice(b * P, (b + 1) * P)
-                quantize(v_codes[h][:, c], v_scales[h][:, c], grouped[b][:])
-
-        gate.append(placed([P, B, P], F32, "gate1", 32))
-        nc.scalar.activation(gate[1][:], og_sb[1][:], SIGMOID)
+            quantize(v_codes[1][:, c], v_scales[1][:, c], v1_grouped[b][:])
 
         def weigh(y, b, codes, scales):
             nc.tensor.matmul_mx(
@@ -228,16 +235,17 @@ def tile_attend_x_sigmoid_gate_kernel(tc, qT, kT, vT, vs, og, offs, out):
                 stop=True,
             )
 
-        y0 = psum.tile([P, B, P], F32, name="y0")
-        for b in range(B):
-            weigh(y0[:, b, :], b, v_codes[0][:, b * P : (b + 1) * P], v_scales[0][:, b * P : (b + 1) * P])
-        y1 = [psum.tile([P, P], F32, name=f"y1_{b}") for b in range(B)]
-        for b in range(B):
-            weigh(y1[b][:], b, v_codes[1][:, b * P : (b + 1) * P], v_scales[1][:, b * P : (b + 1) * P])
-        o0 = keep.tile([P, B, P], F32, name="o0")
-        nc.vector.scalar_tensor_tensor(o0[:], y0[:], 1.0 / 16.0, gate[0][:], MULT, MULT)
-        nc.sync.dma_start(out.rearrange("b q e -> q b e")[:, :, 0:P], o0[:])
-        for b in range(B):
-            o1 = keep.tile([P, P], F32, name=f"o1_{b}")
-            nc.vector.scalar_tensor_tensor(o1[:], y1[b][:], 1.0 / 16.0, gate[1][:, b, :], MULT, MULT)
-            nc.sync.dma_start(out[b, :, P:DV], o1[:])
+        first = psum.tile([P, DV], F32, name="y_first")
+        for h in range(2):
+            weigh(first[:, h * P : (h + 1) * P], 0, v_codes[h][:, 0:P], v_scales[h][:, 0:P])
+        second = [psum.tile([P, P], F32, name=f"y_second{h}") for h in range(2)]
+        for h in range(2):
+            weigh(second[h][:], 1, v_codes[h][:, P : 2 * P], v_scales[h][:, P : 2 * P])
+        o_first = placed([P, DV], F32, "o_first", 31.5)
+        nc.vector.scalar_tensor_tensor(o_first[:], first[:], 1.0 / 16.0, gate[:, 0, :], MULT, MULT)
+        nc.sync.dma_start(out[0], o_first[:])
+        o_second = [placed([P, P], F32, "o_second0", 32.5), keep.tile([P, P], F32, name="o_second1")]
+        for h in range(2):
+            c = slice(h * P, (h + 1) * P)
+            nc.vector.scalar_tensor_tensor(o_second[h][:], second[h][:], 1.0 / 16.0, gate[:, 1, c], MULT, MULT)
+            nc.sync.dma_start(out[1, :, c], o_second[h][:])

@@ -22,8 +22,8 @@ ADD = mybir.AluOpType.add
 FLOPS = 2 * B * NQ * N * (D + DV)
 BYTES = 4 * (B * D * NQ + D * T + DV * T + T + 2 * B * NQ * DV) + 2 * P * (B * N // 16)
 
-KEY_PIECES = [[(0, 1024, 384), (1024, T, 384)], [(0, 1024, 384), (1024, 1664, 240), (1664, T, 144)]]
-ON_VECTOR = 256
+KEY_PIECES = [[(0, 1024, 384), (1024, T, 384)], [(0, 640, 224), (640, 1280, 224), (1280, 1792, 176), (1792, T, 88)]]
+ON_VECTOR = 192
 
 
 def tile_attend_x_sigmoid_gate_kernel(tc, qT, kT, vT, vs, og, offs, out):
@@ -146,6 +146,8 @@ def tile_attend_x_sigmoid_gate_kernel(tc, qT, kT, vT, vs, og, offs, out):
 
         score = [psum.tile([P, PACK, NQ], F32, name=f"score{b}") for b in range(B)]
 
+        query_parts = [[slice(0, NQ // 2), slice(NQ // 2, NQ)], [slice(0, NQ)]]
+
         def scores(b):
             for t in range(PACK):
                 c = slice(t * P, (t + 1) * P)
@@ -160,7 +162,8 @@ def tile_attend_x_sigmoid_gate_kernel(tc, qT, kT, vT, vs, og, offs, out):
                 )
 
         def sigmoid(p_sb, b):
-            nc.scalar.activation(p_sb[:], score[b][:].rearrange("p t q -> p q t"), SIGMOID)
+            for rows in query_parts[b]:
+                nc.scalar.activation(p_sb[:, rows, :], score[b][:].rearrange("p t q -> p q t")[:, rows, :], SIGMOID)
 
         def paired(picked):
             return picked[:].rearrange("p (u m r) -> p m u r", u=2, r=2)
@@ -195,7 +198,8 @@ def tile_attend_x_sigmoid_gate_kernel(tc, qT, kT, vT, vs, og, offs, out):
 
         w_grouped = [keep.tile([P, NQ, PACK], BF16, name=f"w_grouped{b}", align_bytes=64) for b in range(B)]
         for b in range(B):
-            nc.gpsimd.tensor_tensor(w_grouped[b][:], p_sb[b][:], vs_wide[:, b, :, :], MULT)
+            for rows in query_parts[b]:
+                nc.gpsimd.tensor_tensor(w_grouped[b][:, rows, :], p_sb[b][:, rows, :], vs_wide[:, b, rows, :], MULT)
 
         v0_grouped = placed([P, B * P * PACK], BF16, "v0_grouped", 28)
         nc.scalar.copy(

@@ -22,7 +22,7 @@ ADD = mybir.AluOpType.add
 FLOPS = 2 * B * NQ * N * (D + DV)
 BYTES = 4 * (B * D * NQ + D * T + DV * T + T + 2 * B * NQ * DV) + 2 * P * (B * N // 16)
 
-KEY_PIECES = [[(0, 1024, 384), (1024, T, 384)], [(0, 640, 224), (640, 1280, 224), (1280, 1792, 176), (1792, T, 88)]]
+KEY_PIECES = [[(0, 1024, 384), (1024, T, 384)], [(0, 1024, 368), (1024, 1664, 224), (1664, T, 136)]]
 ON_VECTOR = 192
 
 
@@ -180,7 +180,10 @@ def tile_attend_x_sigmoid_gate_kernel(tc, qT, kT, vT, vs, og, offs, out):
 
         scores(0)
         scores(1)
-        v_picked = [[keep.tile([P, N], BF16, name=f"v_picked{h}{b}") for b in range(B)] for h in range(2)]
+        v_picked = [
+            [keep.tile([P, N], BF16, name=f"v_picked0{b}") for b in range(B)],
+            [keep.tile([P, N], BF16, name="v_picked10"), placed([P, N], BF16, "v_picked11", 32)],
+        ]
         nc.scalar.activation(v_picked[0][0][:, ON_VECTOR:N], listed(v_win[0], 0, ON_VECTOR, N), COPY)
         nc.vector.tensor_copy(v_picked[0][0][:, 0:ON_VECTOR], listed(v_win[0], 0, 0, ON_VECTOR))
         nc.vector.tensor_copy(paired(v_picked[0][1]), listed(v_win[0], 1))
@@ -206,17 +209,17 @@ def tile_attend_x_sigmoid_gate_kernel(tc, qT, kT, vT, vs, og, offs, out):
             out=v0_grouped[:].bitcast(F32).rearrange("p (b e u) -> p b e u", b=B, u=2),
             in_=bank0[:].rearrange("p (b u) e -> p b e u", u=2),
         )
-        gate = keep.tile([P, B, DV], F32, name="gate")
-        nc.scalar.activation(gate[:], og_sb[:], SIGMOID)
-        v1_grouped = [
-            keep.tile([P, P * PACK], BF16, name="v1_grouped0", align_bytes=64),
-            placed([P, P * PACK], BF16, "v1_grouped1", 32),
-        ]
+        gate1 = keep.tile([P, B, P], F32, name="gate1")
+        nc.scalar.activation(gate1[:], og_sb[:, :, P:DV], SIGMOID)
+        v1_grouped = [keep.tile([P, P * PACK], BF16, name=f"v1_grouped{b}", align_bytes=64) for b in range(B)]
         for b in range(B):
             nc.scalar.copy(
                 out=v1_grouped[b][:].bitcast(F32).rearrange("p (e u) -> p e u", u=2),
                 in_=bank1[b][:, 0:2, :].rearrange("p u e -> p e u"),
             )
+
+        gate0 = placed([P, B, P], F32, "gate0", 32)
+        nc.scalar.activation(gate0[:], og_sb[:, :, 0:P], SIGMOID)
 
         w_codes = placed([P, B * NQ], U32, "w_codes", 8)
         w_scales = keep.tile([P, B * NQ], U8, name="w_scales", align_bytes=64)
@@ -226,6 +229,8 @@ def tile_attend_x_sigmoid_gate_kernel(tc, qT, kT, vT, vs, og, offs, out):
         for b in range(B):
             c = slice(b * P, (b + 1) * P)
             quantize(w_codes[:, c], w_scales[:, c], w_grouped[b][:].rearrange("p q j -> p (q j)"))
+        for b in range(B):
+            c = slice(b * P, (b + 1) * P)
             quantize(v_codes[1][:, c], v_scales[1][:, c], v1_grouped[b][:])
 
         def weigh(y, b, codes, scales):
@@ -239,17 +244,16 @@ def tile_attend_x_sigmoid_gate_kernel(tc, qT, kT, vT, vs, og, offs, out):
                 stop=True,
             )
 
-        first = psum.tile([P, DV], F32, name="y_first")
-        for h in range(2):
-            weigh(first[:, h * P : (h + 1) * P], 0, v_codes[h][:, 0:P], v_scales[h][:, 0:P])
-        second = [psum.tile([P, P], F32, name=f"y_second{h}") for h in range(2)]
-        for h in range(2):
-            weigh(second[h][:], 1, v_codes[h][:, P : 2 * P], v_scales[h][:, P : 2 * P])
-        o_first = placed([P, DV], F32, "o_first", 31.5)
-        nc.vector.scalar_tensor_tensor(o_first[:], first[:], 1.0 / 16.0, gate[:, 0, :], MULT, MULT)
-        nc.sync.dma_start(out[0], o_first[:])
-        o_second = [placed([P, P], F32, "o_second0", 32.5), keep.tile([P, P], F32, name="o_second1")]
-        for h in range(2):
-            c = slice(h * P, (h + 1) * P)
-            nc.vector.scalar_tensor_tensor(o_second[h][:], second[h][:], 1.0 / 16.0, gate[:, 1, c], MULT, MULT)
-            nc.sync.dma_start(out[1, :, c], o_second[h][:])
+        y0 = psum.tile([P, B, P], F32, name="y0")
+        for b in range(B):
+            weigh(y0[:, b, :], b, v_codes[0][:, b * P : (b + 1) * P], v_scales[0][:, b * P : (b + 1) * P])
+        y1 = [psum.tile([P, P], F32, name=f"y1_{b}") for b in range(B)]
+        for b in range(B):
+            weigh(y1[b][:], b, v_codes[1][:, b * P : (b + 1) * P], v_scales[1][:, b * P : (b + 1) * P])
+        o0 = keep.tile([P, B, P], F32, name="o0")
+        nc.vector.scalar_tensor_tensor(o0[:], y0[:], 1.0 / 16.0, gate0[:], MULT, MULT)
+        nc.sync.dma_start(out.rearrange("b q e -> q b e")[:, :, 0:P], o0[:])
+        for b in range(B):
+            o1 = keep.tile([P, P], F32, name=f"o1_{b}")
+            nc.vector.scalar_tensor_tensor(o1[:], y1[b][:], 1.0 / 16.0, gate1[:, b, :], MULT, MULT)
+            nc.sync.dma_start(out[b, :, P:DV], o1[:])

from contextlib import ExitStack

import concourse.mybir as mybir
from concourse.masks import make_identity

B, N, T, D, DV, NQ = 2, 512, 2048, 512, 256, 128
P = 128
PACK = 4

F32 = mybir.dt.float32
BF16 = mybir.dt.bfloat16
U32 = mybir.dt.uint32
I32 = mybir.dt.int32
U16 = mybir.dt.uint16
U8 = mybir.dt.uint8
FP8X4 = mybir.dt.float8_e4m3fn_x4
SIGMOID = mybir.ActivationFunctionType.Sigmoid
COPY = mybir.ActivationFunctionType.Copy
MULT = mybir.AluOpType.mult
ADD = mybir.AluOpType.add

FLOPS = 2 * B * NQ * N * (D + DV)
BYTES = 4 * (B * D * NQ + D * T + DV * T + T + 2 * B * NQ * DV) + 2 * P * (B * N // 16)

KEY_PIECES = [[(0, 1024, 384), (1024, T, 384)], [(0, 1024, 368), (1024, 1664, 224), (1664, T, 136)]]
ON_VECTOR = 192


def tile_attend_x_sigmoid_gate_kernel(tc, qT, kT, vT, vs, og, offs, out):
    nc = tc.nc
    cols = N // 16
    last = P - 1

    with ExitStack() as ctx:
        keep = ctx.enter_context(tc.tile_pool(name="keep", bufs=1))
        shared = ctx.enter_context(tc.tile_pool(name="shared", bufs=1))
        psum = ctx.enter_context(tc.psum_pool(name="psum", bufs=1))

        def placed(shape, dtype, name, kib):
            return shared.tile(shape, dtype, name=name, offset=int(kib * 1024), align_bytes=64)

        offsets = keep.tile([P, B * N // 16], U16, name="offsets")
        vs_win = keep.tile([P, T], F32, name="vs_win")
        nc.scalar.dma_start(vs_win[last:P, :], vs[0:1, :])
        nc.gpsimd.memset(vs_win[0:last, T // 2 : T], 0.0)
        nc.vector.memset(vs_win[0:last, 0 : T // 2], 0.0)

        nc.sync.dma_start(offsets[:], offs)
        k_rows = kT.rearrange("(p j) t -> p (j t)", j=PACK)
        k_raw = [keep.tile([P, 2 * T], F32, name="k_raw0"), placed([P, 2 * T], F32, "k_raw1", 40)]
        for u in range(2):
            start = 0
            for lo, hi, share in KEY_PIECES[u]:
                nc.sync.dma_start(k_raw[u][:, start : T + hi], k_rows[:, 2 * u * T + start : (2 * u + 1) * T + hi])
                start = T + hi
        q_raw = [keep.tile([P, PACK * NQ], F32, name=f"q_raw{b}") for b in range(B)]
        for b in range(B):
            nc.sync.dma_start(q_raw[b][:], qT[b].rearrange("(p j) q -> p (j q)", j=PACK))
        v_win = [placed([P, T], F32, f"v_win{h}", 8 * h) for h in range(2)]
        for h in range(2):
            nc.sync.dma_start(v_win[h][:], vT[h * P : (h + 1) * P, :])
        og_sb = keep.tile([P, B, DV], F32, name="og_sb")
        nc.sync.dma_start(og_sb[:], og.rearrange("b q e -> q b e"))

        warm = keep.tile([P, 1], F32, name="warm")
        nc.vector.memset(warm[:], 0.0)
        nc.scalar.activation(warm[:], warm[:], SIGMOID)
        ident = keep.tile([P, P], F32, name="ident")
        make_identity(nc, ident[:])

        def listed(window, b, lo=0, hi=N):
            return window[:].indirect(offsets[:, b * cols + lo // 16 : b * cols + hi // 16])

        def quantize(codes, scales, grouped):
            nc.vector.quantize_mx(out=codes.bitcast(FP8X4), scales=scales, in_=grouped)

        def turn_bank():
            return psum.tile([P, PACK, P], F32, name="turned", tag="turned", bufs=2)

        vs_picked = keep.tile([P, B * N], F32, name="vs_picked")
        nc.vector.tensor_copy(vs_picked[:], vs_win[:].indirect(offsets[:]))
        vs_wide = keep.tile([P, B, NQ, PACK], F32, name="vs_wide")
        for b in range(B):
            turned = turn_bank()
            picked = vs_picked[:, b * N : (b + 1) * N].rearrange("p (m t) -> p t m", t=PACK)
            for t in range(PACK):
                nc.tensor.transpose(turned[:, t, :], picked[:, t, :], ident[:])
            nc.scalar.copy(
                out=vs_wide[:, b, :, :],
                in_=turned[:, :, last:P].rearrange("p t o -> p o t").to_broadcast([P, NQ, PACK]),
            )

        k_win = [keep.tile([P, T], U32, name=f"k_win{u}") for u in range(2)]
        half = N // 2
        k_both = [placed([P, 2, N], U32, "k_both0", 20), keep.tile([P, 2, N], U32, name="k_both1")]
        for u in range(2):
            for lo, hi, share in KEY_PIECES[u]:
                pairs = k_win[u][:, lo:hi].bitcast(BF16).rearrange("p (t r) -> p t r", r=2)
                rows = k_raw[u][:].rearrange("p (r t) -> p t r", r=2)[:, lo:hi, :]
                nc.scalar.activation(pairs[:, 0:share, :], rows[:, 0:share, :], COPY)
                nc.vector.tensor_copy(pairs[:, share:, :], rows[:, share:, :])
            for b in range(B):
                step = half if (u, b) == (1, 0) else N
                dealt = k_both[b][:, u, :].rearrange("p (t m) -> p m t", t=PACK)
                for lo in range(0, N, step):
                    nc.vector.tensor_copy(dealt[:, lo // PACK : (lo + step) // PACK, :], listed(k_win[u], b, lo, lo + step))

        q_grouped = placed([P, B, NQ, PACK], BF16, "q_grouped", 40)
        for b in range(B):
            rows = q_raw[b][:].rearrange("p (j q) -> p q j", j=PACK)
            nc.gpsimd.tensor_scalar(q_grouped[:, b, :, :], rows, 1.0, 0.0, MULT, ADD)

        k_grouped0 = keep.tile([P, PACK * N], BF16, name="k_grouped0", align_bytes=64)
        woven = k_grouped0[:].bitcast(U32).rearrange("p (t m u) -> p t m u", t=PACK, u=2)
        words = k_both[0][:].rearrange("p u (t m) -> p t m u", t=PACK)
        for lo in range(0, P, P // 2):
            nc.scalar.copy(out=woven[:, :, lo : lo + P // 2, :], in_=words[:, :, lo : lo + P // 2, :])

        q_codes = [keep.tile([P, NQ], U32, name="q_codes0", align_bytes=64), placed([P, NQ], U32, "q_codes1", 22)]
        q_scales = keep.tile([P, B * NQ], U8, name="q_scales", align_bytes=64)
        k_codes = [keep.tile([P, N], U32, name="k_codes0", align_bytes=64), placed([P, N], U32, "k_codes1", 28)]
        k_scales = [keep.tile([P, N], U8, name=f"k_scales{b}", align_bytes=64) for b in range(B)]

        def quantize_queries(b):
            c = slice(b * NQ, (b + 1) * NQ)
            quantize(q_codes[b][:], q_scales[:, c], q_grouped[:, b, :, :].rearrange("p q j -> p (q j)"))

        quantize_queries(0)
        quantize(k_codes[0][:], k_scales[0][:], k_grouped0[:])
        k_grouped1 = [
            keep.tile([P, PACK * half], BF16, name="k_grouped1a", align_bytes=64),
            placed([P, PACK * half], BF16, "k_grouped1b", 20),
        ]
        nc.scalar.copy(
            out=k_grouped1[0][:].bitcast(U32).rearrange("p (c u) -> p c u", u=2),
            in_=k_both[1][:, :, 0:half].rearrange("p u c -> p c u"),
        )
        nc.vector.tensor_copy(
            k_grouped1[1][:].bitcast(I32).rearrange("p (c u) -> p c u", u=2),
            k_both[1][:, :, half:N].bitcast(I32).rearrange("p u c -> p c u"),
        )
        quantize_queries(1)
        for c in range(2):
            part = slice(c * half, (c + 1) * half)
            quantize(k_codes[1][:, part], k_scales[1][:, part], k_grouped1[c][:])

        score = [psum.tile([P, PACK, NQ], F32, name=f"score{b}") for b in range(B)]

        query_parts = [[slice(0, NQ // 2), slice(NQ // 2, NQ)], [slice(0, NQ)]]

        def scores(b):
            for t in range(PACK):
                c = slice(t * P, (t + 1) * P)
                nc.tensor.matmul_mx(
                    out=score[b][:, t, :],
                    lhsT=k_codes[b][:, c].bitcast(FP8X4),
                    lhsT_scale=k_scales[b][:, c],
                    rhs=q_codes[b][:].bitcast(FP8X4),
                    rhs_scale=q_scales[:, b * NQ : (b + 1) * NQ],
                    start=True,
                    stop=True,
                )

        def sigmoid(p_sb, b):
            for rows in query_parts[b]:
                nc.scalar.activation(p_sb[:, rows, :], score[b][:].rearrange("p t q -> p q t")[:, rows, :], SIGMOID)

        def paired(picked):
            return picked[:].rearrange("p (u m r) -> p m u r", u=2, r=2)

        def turn_in_order(bank, picked):
            words = picked[:].bitcast(F32).rearrange("p (m u) -> p u m", u=2)
            for u in range(2):
                nc.tensor.transpose(bank[:, u, :], words[:, u, :], ident[:])

        def turn_paired(bank, picked):
            words = picked[:].bitcast(F32)
            for u in range(2):
                nc.tensor.transpose(bank[:, u, :], words[:, u * P : (u + 1) * P], ident[:])

        scores(0)
        scores(1)
        v_picked = [
            [keep.tile([P, N], BF16, name=f"v_picked0{b}") for b in range(B)],
            [keep.tile([P, N], BF16, name="v_picked10"), placed([P, N], BF16, "v_picked11", 32)],
        ]
        nc.scalar.activation(v_picked[0][0][:, ON_VECTOR:N], listed(v_win[0], 0, ON_VECTOR, N), COPY)
        nc.vector.tensor_copy(v_picked[0][0][:, 0:ON_VECTOR], listed(v_win[0], 0, 0, ON_VECTOR))
        nc.vector.tensor_copy(paired(v_picked[0][1]), listed(v_win[0], 1))
        p_sb = [keep.tile([P, NQ, PACK], F32, name=f"p{b}") for b in range(B)]
        for b in range(B):
            sigmoid(p_sb[b], b)
        bank0 = psum.tile([P, PACK, P], F32, name="bank0")
        turn_in_order(bank0[:, 0:2, :], v_picked[0][0])
        turn_paired(bank0[:, 2:4, :], v_picked[0][1])

        bank1 = [turn_bank() for b in range(B)]
        for b in range(B):
            nc.vector.tensor_copy(paired(v_picked[1][b]), listed(v_win[1], b))
            turn_paired(bank1[b], v_picked[1][b])

        w_grouped = [keep.tile([P, NQ, PACK], BF16, name=f"w_grouped{b}", align_bytes=64) for b in range(B)]
        for b in range(B):
            for rows in query_parts[b]:
                nc.gpsimd.tensor_tensor(w_grouped[b][:, rows, :], p_sb[b][:, rows, :], vs_wide[:, b, rows, :], MULT)

        v0_grouped = placed([P, B * P * PACK], BF16, "v0_grouped", 28)
        nc.scalar.copy(
            out=v0_grouped[:].bitcast(F32).rearrange("p (b e u) -> p b e u", b=B, u=2),
            in_=bank0[:].rearrange("p (b u) e -> p b e u", u=2),
        )
        gate1 = keep.tile([P, B, P], F32, name="gate1")
        nc.scalar.activation(gate1[:], og_sb[:, :, P:DV], SIGMOID)
        v1_grouped = [keep.tile([P, P * PACK], BF16, name=f"v1_grouped{b}", align_bytes=64) for b in range(B)]
        for b in range(B):
            nc.scalar.copy(
                out=v1_grouped[b][:].bitcast(F32).rearrange("p (e u) -> p e u", u=2),
                in_=bank1[b][:, 0:2, :].rearrange("p u e -> p e u"),
            )

        gate0 = placed([P, B, P], F32, "gate0", 32)
        nc.scalar.activation(gate0[:], og_sb[:, :, 0:P], SIGMOID)

        w_codes = placed([P, B * NQ], U32, "w_codes", 8)
        w_scales = keep.tile([P, B * NQ], U8, name="w_scales", align_bytes=64)
        v_codes = [placed([P, B * P], U32, "v_codes0", 10), keep.tile([P, B * P], U32, name="v_codes1", align_bytes=64)]
        v_scales = [keep.tile([P, B * P], U8, name=f"v_scales{h}", align_bytes=64) for h in range(2)]
        quantize(v_codes[0][:], v_scales[0][:], v0_grouped[:])
        for b in range(B):
            c = slice(b * P, (b + 1) * P)
            quantize(w_codes[:, c], w_scales[:, c], w_grouped[b][:].rearrange("p q j -> p (q j)"))
        for b in range(B):
            c = slice(b * P, (b + 1) * P)
            quantize(v_codes[1][:, c], v_scales[1][:, c], v1_grouped[b][:])

        def weigh(y, b, codes, scales):
            nc.tensor.matmul_mx(
                out=y,
                lhsT=w_codes[:, b * NQ : (b + 1) * NQ].bitcast(FP8X4),
                lhsT_scale=w_scales[:, b * NQ : (b + 1) * NQ],
                rhs=codes.bitcast(FP8X4),
                rhs_scale=scales,
                start=True,
                stop=True,
            )

        y0 = psum.tile([P, B, P], F32, name="y0")
        for b in range(B):
            weigh(y0[:, b, :], b, v_codes[0][:, b * P : (b + 1) * P], v_scales[0][:, b * P : (b + 1) * P])
        y1 = [psum.tile([P, P], F32, name=f"y1_{b}") for b in range(B)]
        for b in range(B):
            weigh(y1[b][:], b, v_codes[1][:, b * P : (b + 1) * P], v_scales[1][:, b * P : (b + 1) * P])
        o0 = keep.tile([P, B, P], F32, name="o0")
        nc.vector.scalar_tensor_tensor(o0[:], y0[:], 1.0 / 16.0, gate0[:], MULT, MULT)
        nc.sync.dma_start(out.rearrange("b q e -> q b e")[:, :, 0:P], o0[:])
        for b in range(B):
            o1 = keep.tile([P, P], F32, name=f"o1_{b}")
            nc.vector.scalar_tensor_tensor(o1[:], y1[b][:], 1.0 / 16.0, gate1[:, b, :], MULT, MULT)
            nc.sync.dma_start(out[b, :, P:DV], o1[:])
